import numpy as np
import ml_dtypes


def mxq(x, axis, fmt="e4m3"):
    dtype, down = {"e4m3": (ml_dtypes.float8_e4m3fn, 7), "e5m2": (ml_dtypes.float8_e5m2, 14)}[fmt]
    v = np.moveaxis(np.asarray(x, np.float32).astype(ml_dtypes.bfloat16).astype(np.float64), axis, -1)
    blocks = v.reshape(v.shape[:-1] + (-1, 32))
    amax = np.abs(blocks).max(-1, keepdims=True)
    byte = np.maximum(np.where(amax > 0, np.frexp(amax)[1] - 1 + 127, 0) - down, 1)
    scale = np.exp2(byte - 127.0)
    codes = (blocks / scale).astype(np.float32).astype(dtype).astype(np.float64)
    return np.moveaxis((codes * scale).reshape(v.shape), -1, axis)


WIDE = False


def mx_kscale(k):
    if not WIDE:
        return np.ones(k)
    levels = np.array([10, -10, 5, -5, 0])
    if k % 512:
        return np.exp2(np.random.permutation(np.resize(levels, k // 32))).repeat(32)
    a = np.empty((k // 512, 16))
    for p in range(k // 512):
        a[p, :8] = np.random.permutation(np.resize(levels, 8))
        for g in range(8):
            far = levels[np.abs(levels - a[p, g]) >= 10]
            a[p, g + 8] = far[np.random.randint(len(far))]
    return np.exp2(a.ravel()).repeat(32)


BF16 = ml_dtypes.bfloat16


def bf(x):
    return np.asarray(x, np.float32).astype(BF16)


def f64(x):
    return np.asarray(x).astype(np.float64)


E2M1 = np.array([0.0, 0.5, 1.0, 1.5, 2.0, 3.0, 4.0, 6.0, -0.0, -0.5, -1.0, -1.5, -2.0, -3.0, -4.0, -6.0])


def pack_weight(w, fmt):
    k, n = w.shape
    w = f64(bf(w)).reshape(k // 32, 32, n)
    amax = np.abs(w).max(1)
    if fmt == "e4m3":
        byte = np.frexp(amax)[1] - 1 + 127 - 7
    else:
        mant, ex = np.frexp(amax / 6.0)
        byte = np.where(mant > 0.5, ex, ex - 1) + 127
    byte = np.clip(np.where(amax > 0, byte, 1), 1, 254)
    scaled = (w * np.exp2(127.0 - byte)[:, None, :]).reshape(k, n).astype(np.float32)
    by_word = np.ascontiguousarray(scaled.reshape(k // 512, 128, 4, n).transpose(0, 1, 3, 2))
    if fmt == "e4m3":
        words = by_word.astype(ml_dtypes.float8_e4m3fn).view(np.uint8)
    else:
        c = by_word.astype(ml_dtypes.float4_e2m1fn).view(np.uint8) & 0xF
        words = c[..., 0::2] | (c[..., 1::2] << 4)
    return np.ascontiguousarray(words), np.ascontiguousarray(byte.astype(np.uint8).reshape(k // 512, 16, n))


def unpack_weight(words, scales, fmt):
    g, p, n, _ = words.shape
    if fmt == "e4m3":
        vals = np.ascontiguousarray(words).view(ml_dtypes.float8_e4m3fn).astype(np.float64)
    else:
        nib = np.empty((g, p, n, 4), np.uint8)
        nib[..., 0::2] = words & 0xF
        nib[..., 1::2] = words >> 4
        vals = E2M1[nib]
    vals = vals * np.repeat(np.exp2(scales.astype(np.float64) - 127.0), 8, axis=1)[..., None]
    return vals.transpose(0, 1, 3, 2).reshape(g * 512, n)
def pack4(w):
    words, scales = pack_weight(w, "e2m1")
    return words.reshape(words.shape[0], 128, -1), scales


def unpack4(words, scales):
    return unpack_weight(words.reshape(words.shape[0], 128, -1, 2), scales, "e2m1")


def planes(Y):
    n, m = Y.shape
    b = f64(bf(Y)).reshape(n // 32, 32, m)
    amax = np.abs(b).max(1)
    byte = np.clip(np.where(amax > 0, np.frexp(amax)[1] - 1 + 127 - 7, 1), 1, 254)
    codes = (b * np.exp2(127.0 - byte)[:, None, :]).reshape(n, m).astype(np.float32).astype(ml_dtypes.float8_e4m3fn).view(np.uint8)
    words = codes.reshape(n // 512, 128, 4, m).transpose(0, 1, 3, 2)
    return np.ascontiguousarray(words), np.ascontiguousarray(byte.astype(np.uint8).reshape(n // 512, 16, m))


R, T, F, E, TURN = 512, 2048, 1024, 1024, 64

def setup_inputs():
    rn = np.random.randn
    s, tm, td = mx_kscale(T), mx_kscale(F), mx_kscale(F)
    offset = np.repeat(rn(T // TURN, F), TURN, axis=0)
    spread = np.exp(0.4 * np.repeat(rn(T // TURN, F), TURN, axis=0))
    raw = 0.3 * rn(F) + offset + spread * rn(T, F)
    rec_mean = raw.mean(axis=0)
    x = raw - rec_mean
    a = np.exp(1.2 * np.repeat(rn(R, T // TURN), TURN, axis=1) + 0.5 * rn(R, T))
    a = a / a.sum(axis=1, keepdims=True)
    attn_words, attn_scales = pack4((a / s).T)
    frame_words, frame_scales = pack4(x * s[:, None] * tm)
    square_words, square_scales = pack4(x * x * s[:, None] * td ** 2)
    return {"attn_words": attn_words, "attn_scales": attn_scales,
            "frame_words": frame_words, "frame_scales": frame_scales,
            "square_words": square_words, "square_scales": square_scales,
            "rec_mean": bf(rec_mean * tm),
            "var_offset": bf(0.3 * np.exp(0.3 * rn(F)) * td ** 2),
            "w_mean": bf(1.2 * rn(F, E) / np.sqrt(F) / tm[:, None]),
            "w_dev": bf(0.5 * rn(F, E) / np.sqrt(F) / td[:, None]),
            "bias": bf(0.3 * rn(E)),
            "gain": bf(np.exp(0.8 * rn(E)))}

def reference(attn_words, attn_scales, frame_words, frame_scales, square_words, square_scales,
              rec_mean, var_offset, w_mean, w_dev, bias, gain):
    P = unpack4(attn_words, attn_scales)
    X = unpack4(frame_words, frame_scales)
    S = unpack4(square_words, square_scales)
    mean = (P.T @ X) + f64(rec_mean)
    dev = np.sqrt((P.T @ S) + f64(var_offset))
    from_mean = mxq(mean, 1, "e4m3") @ mxq(f64(w_mean), 0, "e4m3")
    from_dev = mxq(dev, 1, "e4m3") @ mxq(f64(w_dev), 0, "e4m3")
    y = np.tanh(from_mean + from_dev + f64(bias)) * f64(gain)
    Y = y.T
    words, scales = planes(Y)
    return y, words, scales

@@ -1,0 +1,358 @@
+from contextlib import ExitStack
+
+import concourse.mybir as mybir
+from concourse.masks import make_identity
+
+R, T, F, E = 512, 2048, 1024, 1024
+FLOPS = 2 * R * T * F * 2 + 2 * R * F * E * 2
+
+F32 = mybir.dt.float32
+BF16 = mybir.dt.bfloat16
+I32 = mybir.dt.int32
+U32 = mybir.dt.uint32
+U8 = mybir.dt.uint8
+FP4X4 = mybir.dt.float4_e2m1fn_x4
+FP8X4 = mybir.dt.float8_e4m3fn_x4
+ACT = mybir.ActivationFunctionType
+ALU = mybir.AluOpType
+
+P = 128
+G = T // 512
+
+
+def tile_speaker_pooled_mean_deviation_k5_kernel(
+    tc, attn_words, attn_scales, frame_words, frame_scales, square_words, square_scales,
+    rec_mean, var_offset, w_mean, w_dev, bias, gain, out_0, out_1, out_2,
+):
+    nc = tc.nc
+    with ExitStack() as ctx:
+        sb = ctx.enter_context(tc.tile_pool(name="sb", bufs=1))
+        psum = ctx.enter_context(tc.psum_pool(name="psum", bufs=1))
+        ctx.enter_context(tc.manual_schedule())
+
+        def tile(name, shape, dtype, tag="", bufs=None):
+            return sb.tile(shape, dtype, name=name, tag=tag, bufs=bufs, align_bytes=64)
+
+        bank = [psum.tile([P, 512], F32, name="bank%d" % i) for i in range(8)]
+
+        attn_first = tile("attn_first", [P, 1, 1024], U8)
+        attn_rest = tile("attn_rest", [P, 3, 1024], U8)
+        attn_plane = tile("attn_plane", [P, G, 512], U8)
+        words_in = {"dev": square_words, "mean": frame_words}
+        scales_in = {"dev": square_scales, "mean": frame_scales}
+        w_in = {"dev": w_dev, "mean": w_mean}
+        plane_raw = {s: tile("plane_raw_" + s, [P, G, 1024], U8) for s in words_in}
+        plane = {}
+        words_raw = {}
+        words = {}
+        w_raw = {}
+        w_grouped = {}
+        w_codes = {}
+        w_plane = {}
+        act_rows = {}
+        act_grouped = {}
+        act_codes = {}
+        act_plane = {}
+
+        def attn(g):
+            src = attn_first[:, 0, :] if g == 0 else attn_rest[:, g - 1, :]
+            return src.bitcast(FP4X4)
+
+        def load_plane(dst, src):
+            rows = src.rearrange("g (q r) n -> r q g n", r=4)
+            for r in range(4):
+                nc.sync.dma_start(out=dst[r:P:32, :, :].bitcast(I32), in_=rows[r].bitcast(I32))
+
+        def load_words(s, h, g0, g1):
+            raw = tile("words_raw_%s_%d_%d" % (s, h, g0), [P, g1 - g0, 1024], U8)
+            words_raw[s, h, g0] = raw
+            src = words_in[s][g0:g1, :, 1024 * h : 1024 * (h + 1)].rearrange("g p n -> p g n")
+            nc.sync.dma_start(out=raw[:].bitcast(I32), in_=src.bitcast(I32))
+
+        def order_words(s, h, g0, g1):
+            dst = tile("words_%s_%d_%d" % (s, h, g0), [P, 4, g1 - g0, 256], U8)
+            for g in range(g0, g1):
+                for j in range(4):
+                    words[s, h, j, g] = dst[:, j, g - g0, :]
+            nc.vector.tensor_copy(
+                out=dst[:].bitcast(I32).rearrange("p j g (q w) -> p j (g q) w", w=2),
+                in_=words_raw[s, h, g0][:].bitcast(I32).rearrange("p g (q j w) -> p j (g q) w", j=4, w=2),
+            )
+
+        def order_plane(s, g0, g1):
+            dst = tile("plane_%s_%d" % (s, g0), [P, 4, g1 - g0, 256], U8)
+            for g in range(g0, g1):
+                for h in range(2):
+                    for j in range(4):
+                        plane[s, h, j, g] = dst[:, j, g - g0, 128 * h : 128 * (h + 1)]
+            nc.vector.tensor_copy(
+                out=dst[:].bitcast(I32).rearrange("p j g q -> p (g q) j"),
+                in_=plane_raw[s][:, g0:g1, :].bitcast(I32).rearrange("p g (q j) -> p (g q) j", j=4),
+            )
+
+        def load_w(s, h, e0, e1):
+            raw = tile("w_raw_%s_%d_%d" % (s, h, e0), [P, 4, 512 * (e1 - e0)], BF16)
+            for e in range(e0, e1):
+                w_raw[s, h, e] = raw[:, :, 512 * (e - e0) : 512 * (e - e0 + 1)]
+            rows = w_in[s][512 * h : 512 * (h + 1), 512 * e0 : 512 * e1].rearrange("(q j c) e -> c q j e", j=4, c=4)
+            for c in range(4):
+                nc.sync.dma_start(out=raw[c:P:4, :, :], in_=rows[c])
+
+        def group_w(engine, s, h, e):
+            dst = tile("w_grouped_%s_%d_%d" % (s, h, e), [P, 4, P, 4], BF16, "w_grouped", 4)
+            w_grouped[s, h, e] = dst
+            src = w_raw[s, h, e].rearrange("p j (m t) -> p t m j", t=4)
+            if engine == "vector":
+                nc.vector.tensor_copy(out=dst[:], in_=src)
+            else:
+                nc.scalar.copy(out=dst[:], in_=src)
+
+        def quantize(codes, scales, grouped):
+            nc.vector.quantize_mx(out=codes.bitcast(FP8X4), scales=scales, in_=grouped)
+
+        def quantize_w(s, h, e):
+            w_codes[s, h, e] = tile("w_codes_%s_%d_%d" % (s, h, e), [P, 512], U32)
+            w_plane[s, h, e] = tile("w_plane_%s_%d_%d" % (s, h, e), [P, 512], U8)
+            quantize(w_codes[s, h, e][:], w_plane[s, h, e][:], w_grouped[s, h, e][:].rearrange("p t m j -> p (t m j)"))
+
+        def pool_pass(s, h, j, g):
+            nc.tensor.matmul_mx(
+                out=bank[4 * h + j][:],
+                lhsT=words[s, h, j, g].bitcast(FP4X4), lhsT_scale=plane[s, h, j, g],
+                rhs=attn(g), rhs_scale=attn_plane[:, g, :],
+                start=(g == 0), stop=(g == G - 1),
+            )
+
+        def pool_group(s, h, j):
+            for g in range(G):
+                pool_pass(s, h, j, g)
+
+        def finish_pool(s, h, j):
+            if j == 0:
+                act_rows[s, h] = tile("act_rows_%s_%d" % (s, h), [P, 4, R], BF16, "act_rows", 2)
+            col = (4 if s == "dev" else 0) + j
+            nc.scalar.activation(
+                out=act_rows[s, h][:, j, :], in_=bank[4 * h + j][:],
+                func=ACT.Sqrt if s == "dev" else ACT.Identity, bias=offsets[:, h, col : col + 1],
+            )
+
+        def group_act(s, h):
+            act_grouped[s, h] = tile("act_grouped_%s_%d" % (s, h), [P, R, 4], BF16, "act_grouped", 2)
+            nc.vector.tensor_copy(out=act_grouped[s, h][:], in_=act_rows[s, h][:].rearrange("p j r -> p r j"))
+
+        def quantize_act(s, h):
+            act_codes[s, h] = tile("act_codes_%s_%d" % (s, h), [P, R], U32)
+            act_plane[s, h] = tile("act_plane_%s_%d" % (s, h), [P, R], U8)
+            quantize(act_codes[s, h][:], act_plane[s, h][:], act_grouped[s, h][:].rearrange("p r j -> p (r j)"))
+
+        passes = [("dev", 0), ("dev", 1), ("mean", 0), ("mean", 1)]
+
+        def embed_pass(acc, e, t, rows, i):
+            s, h = passes[i]
+            cols = slice(P * t, P * (t + 1))
+            nc.tensor.matmul_mx(
+                out=acc,
+                lhsT=w_codes[s, h, e][:, cols].bitcast(FP8X4), lhsT_scale=w_plane[s, h, e][:, cols],
+                rhs=act_codes[s, h][:, rows].bitcast(FP8X4), rhs_scale=act_plane[s, h][:, rows],
+                start=(i == 0), stop=(i == 3),
+            )
+
+        squashed = [tile("squashed%d" % e, [P, 4, R], F32) for e in range(2)]
+        y_t = [tile("y_t%d" % e, [P, 4, R], F32) for e in range(2)]
+        y_grouped = [tile("y_grouped%d" % e, [P, R, 4], BF16) for e in range(2)]
+        y_codes = [tile("y_codes%d" % e, [P, R], U32) for e in range(2)]
+        y_plane = tile("y_plane", [P, 2, R], U8)
+        y_rows = [tile("y_rows%d" % e, [P, 4, 512], F32) for e in range(2)]
+
+        def squash(acc, e, t, rows):
+            nc.scalar.activation(out=squashed[e][:, t, rows], in_=acc, func=ACT.Tanh, bias=bias_f[:, 4 * e + t : 4 * e + t + 1])
+
+        def apply_gain(e, t, rows):
+            nc.vector.tensor_scalar(
+                out=y_t[e][:, t, rows], in0=squashed[e][:, t, rows],
+                scalar1=gain_f[:, 4 * e + t : 4 * e + t + 1], scalar2=None, op0=ALU.mult,
+            )
+
+        def group_y(e, rows):
+            nc.vector.tensor_copy(out=y_grouped[e][:, rows, :], in_=y_t[e][:, :, rows].rearrange("p t r -> p r t"))
+
+        def quantize_y(e, rows):
+            quantize(y_codes[e][:, rows], y_plane[:, e, rows], y_grouped[e][:, rows, :].rearrange("p r t -> p (r t)"))
+
+        def turn(b, e, rb):
+            for t in range(4):
+                nc.tensor.transpose(bank[b][:, P * t : P * (t + 1)], y_t[e][:, t, P * rb : P * (rb + 1)], ident[:])
+
+        def unload(engine, b, e, rb):
+            dst = y_rows[e][:, rb, :].rearrange("p (m t) -> p m t", t=4)
+            src = bank[b][:].rearrange("p (t m) -> p m t", t=4)
+            if engine == "vector":
+                nc.vector.tensor_copy(out=dst, in_=src)
+            else:
+                nc.scalar.copy(out=dst, in_=src)
+
+        def store_rows(queue, e, rb0, rb1):
+            dst = out_0[P * rb0 : P * rb1, 512 * e : 512 * (e + 1)].rearrange("(b p) n -> p b n", p=P)
+            queue.dma_start(out=dst, in_=y_rows[e][:, rb0:rb1, :])
+
+        def store_codes(queue, e, rows):
+            dst = out_1[e].rearrange("p m t -> p (m t)").bitcast(I32)
+            queue.dma_start(out=dst[:, rows], in_=y_codes[e][:, rows].bitcast(I32))
+
+        vec_rows = tile("vec_rows", [8, 256], BF16)
+        vec_f = tile("vec_f", [P, 256], F32)
+        offsets = tile("offsets", [P, 2, 8], F32)
+        bias_b = tile("bias_b", [P, 2, 4], BF16)
+        gain_b = tile("gain_b", [P, 2, 4], BF16)
+        bias_f = tile("bias_f", [P, 8], F32)
+        gain_f = tile("gain_f", [P, 8], F32)
+        ident = tile("ident", [P, P], F32)
+        warm = tile("warm", [P, 8], F32)
+
+        nc.vector.memset(attn_plane[:].bitcast(I32), 0)
+        nc.vector.memset(plane_raw["dev"][:].bitcast(I32), 0)
+        nc.vector.memset(warm[:, 0:1], 1.0)
+        nc.vector.memset(plane_raw["mean"][:].bitcast(I32), 0)
+        nc.scalar.dma_start(out=vec_rows[4:8, :].rearrange("j (q c) -> j q c", c=4), in_=var_offset.rearrange("(q j c) -> j q c", j=4, c=4))
+        nc.scalar.dma_start(out=vec_rows[0:4, :].rearrange("j (q c) -> j q c", c=4), in_=rec_mean.rearrange("(q j c) -> j q c", j=4, c=4))
+        nc.scalar.activation(out=warm[:, 1:2], in_=warm[:, 0:1], func=ACT.Sqrt)
+        nc.gpsimd.memset(vec_f[:], 0.0)
+        make_identity(nc, ident[:])
+
+        nc.sync.dma_start(out=attn_first[:].bitcast(I32), in_=attn_words[0:1].rearrange("g p n -> p g n").bitcast(I32))
+        load_words("dev", 0, 0, 1)
+        load_plane(attn_plane, attn_scales)
+        load_plane(plane_raw["dev"], square_scales)
+        nc.sync.dma_start(out=attn_rest[:].bitcast(I32), in_=attn_words[1:4].rearrange("g p n -> p g n").bitcast(I32))
+        load_words("dev", 0, 1, 4)
+        load_w("dev", 0, 0, 1)
+        load_words("dev", 1, 0, 4)
+        load_w("dev", 1, 0, 1)
+        load_plane(plane_raw["mean"], frame_scales)
+        load_words("mean", 0, 0, 4)
+        load_w("mean", 0, 0, 1)
+        load_words("mean", 1, 0, 4)
+        load_w("mean", 1, 0, 1)
+        nc.sync.dma_start(out=bias_b[:], in_=bias.rearrange("(e p t) -> p e t", e=2, t=4))
+        nc.sync.dma_start(out=gain_b[:], in_=gain.rearrange("(e p t) -> p e t", e=2, t=4))
+        load_w("dev", 0, 1, 2)
+        load_w("dev", 1, 1, 2)
+        load_w("mean", 0, 1, 2)
+        load_w("mean", 1, 1, 2)
+
+        order_words("dev", 0, 0, 1)
+        order_plane("dev", 0, 1)
+        for j in range(4):
+            pool_pass("dev", 0, j, 0)
+        order_plane("dev", 1, 4)
+        order_words("dev", 0, 1, 4)
+        nc.vector.tensor_copy(out=vec_f[0:8, :], in_=vec_rows[:])
+        for j in range(4):
+            pool_pass("dev", 0, j, 1)
+        for h in range(2):
+            nc.tensor.transpose(bank[7][:, P * h : P * (h + 1)], vec_f[:, P * h : P * (h + 1)], ident[:])
+        nc.vector.tensor_copy(out=offsets[:], in_=bank[7][:, 0:256].rearrange("p (h v) -> p h v", h=2)[:, :, 0:8])
+        for g in range(2, 4):
+            for j in range(4):
+                pool_pass("dev", 0, j, g)
+        group_w("scalar", "dev", 0, 0)
+        order_words("dev", 1, 0, 4)
+        for j in range(4):
+            finish_pool("dev", 0, j)
+        for j in range(4):
+            pool_group("dev", 1, j)
+        group_w("vector", "dev", 1, 0)
+        quantize_w("dev", 0, 0)
+        order_plane("mean", 0, 4)
+        quantize_w("dev", 1, 0)
+        order_words("mean", 0, 0, 4)
+        group_act("dev", 0)
+        group_w("scalar", "mean", 0, 0)
+        for j in range(4):
+            finish_pool("dev", 1, j)
+        for j in range(4):
+            pool_group("mean", 0, j)
+        order_words("mean", 1, 0, 4)
+        quantize_act("dev", 0)
+        group_w("vector", "mean", 1, 0)
+        quantize_w("mean", 0, 0)
+        group_act("dev", 1)
+        quantize_w("mean", 1, 0)
+        group_w("scalar", "dev", 0, 1)
+        for j in range(4):
+            finish_pool("mean", 0, j)
+        for j in range(4):
+            pool_group("mean", 1, j)
+        nc.vector.tensor_copy(out=bias_f[:], in_=bias_b[:].rearrange("p e t -> p (e t)"))
+        nc.vector.tensor_copy(out=gain_f[:], in_=gain_b[:].rearrange("p e t -> p (e t)"))
+        group_w("vector", "dev", 1, 1)
+        quantize_act("dev", 1)
+        group_w("vector", "mean", 0, 1)
+        quantize_w("dev", 0, 1)
+        group_act("mean", 0)
+        quantize_w("dev", 1, 1)
+        quantize_act("mean", 0)
+        for j in range(4):
+            finish_pool("mean", 1, j)
+        group_w("vector", "mean", 1, 1)
+        group_act("mean", 1)
+        quantize_w("mean", 0, 1)
+        quantize_act("mean", 1)
+        quantize_w("mean", 1, 1)
+
+        whole = slice(0, R)
+        halves = [slice(0, 256), slice(256, 512)]
+        for i in range(4):
+            for t in range(4):
+                embed_pass(bank[t][:], 0, t, whole, i)
+        for t in range(4):
+            squash(bank[t][:], 0, t, whole)
+            apply_gain(0, t, whole)
+
+        def half_acc(u, t):
+            return bank[4 + 2 * u + t // 2][:, 256 * (t % 2) : 256 * (t % 2 + 1)]
+
+        def embed_half(u):
+            for t in range(4):
+                for i in range(4):
+                    embed_pass(half_acc(u, t), 1, t, halves[u], i)
+
+        embed_half(0)
+        for rb in range(4):
+            turn(rb, 0, rb)
+        group_y(0, whole)
+        for t in range(4):
+            squash(half_acc(0, t), 1, t, halves[0])
+            apply_gain(1, t, halves[0])
+        quantize_y(0, whole)
+        store_codes(nc.sync, 0, whole)
+        embed_half(1)
+        unload("scalar", 0, 0, 0)
+        unload("vector", 1, 0, 1)
+        unload("scalar", 2, 0, 2)
+        store_rows(nc.sync, 0, 0, 2)
+        group_y(1, halves[0])
+        unload("scalar", 3, 0, 3)
+        store_rows(nc.sync, 0, 2, 4)
+        quantize_y(1, halves[0])
+        store_codes(nc.sync, 1, halves[0])
+        for t in range(4):
+            squash(half_acc(1, t), 1, t, halves[1])
+            apply_gain(1, t, halves[1])
+        turn(0, 1, 0)
+        turn(1, 1, 1)
+        turn(2, 1, 2)
+        turn(3, 1, 3)
+        unload("scalar", 0, 1, 0)
+        group_y(1, halves[1])
+        unload("scalar", 1, 1, 1)
+        store_rows(nc.sync, 1, 0, 2)
+        quantize_y(1, halves[1])
+        unload("scalar", 2, 1, 2)
+        store_codes(nc.sync, 1, halves[1])
+        plane_rows = out_2.rearrange("g (q r) m -> r q g m", r=4)
+        for r in range(4):
+            nc.sync.dma_start(out=plane_rows[r].bitcast(I32), in_=y_plane[r:P:32, :, :].bitcast(I32))
+        unload("vector", 3, 1, 3)
+        store_rows(nc.scalar, 1, 2, 3)
+        store_rows(nc.sync, 1, 3, 4)

@@ -101,11 +101,12 @@ def tile_speaker_pooled_mean_deviation_k5_kernel(
         def group_w(engine, s, h, e):
             dst = tile("w_grouped_%s_%d_%d" % (s, h, e), [P, 4, P, 4], BF16, "w_grouped", 4)
             w_grouped[s, h, e] = dst
-            src = w_raw[s, h, e].rearrange("p j (m t) -> p t m j", t=4)
+            src = w_raw[s, h, e].rearrange("p j (m a t) -> p m t a j", a=2, t=4)
+            out = dst[:].rearrange("p t (m a) j -> p m t a j", a=2)
             if engine == "vector":
-                nc.vector.tensor_copy(out=dst[:], in_=src)
+                nc.vector.tensor_copy(out=out, in_=src)
             else:
-                nc.scalar.copy(out=dst[:], in_=src)
+                nc.scalar.copy(out=out, in_=src)
 
         def quantize(codes, scales, grouped):
             nc.vector.quantize_mx(out=codes.bitcast(FP8X4), scales=scales, in_=grouped)
@@ -130,15 +131,18 @@ def tile_speaker_pooled_mean_deviation_k5_kernel(
         def finish_pool(s, h, j):
             if j == 0:
                 act_rows[s, h] = tile("act_rows_%s_%d" % (s, h), [P, 4, R], BF16, "act_rows", 2)
-            col = (4 if s == "dev" else 0) + j
+            col = (2 if s == "dev" else 0) + h
             nc.scalar.activation(
                 out=act_rows[s, h][:, j, :], in_=bank[4 * h + j][:],
-                func=ACT.Sqrt if s == "dev" else ACT.Identity, bias=offsets[:, h, col : col + 1],
+                func=ACT.Sqrt if s == "dev" else ACT.Identity, bias=vecs[:, j, col : col + 1],
             )
 
         def group_act(s, h):
             act_grouped[s, h] = tile("act_grouped_%s_%d" % (s, h), [P, R, 4], BF16, "act_grouped", 2)
-            nc.vector.tensor_copy(out=act_grouped[s, h][:], in_=act_rows[s, h][:].rearrange("p j r -> p r j"))
+            nc.vector.tensor_copy(
+                out=act_grouped[s, h][:].rearrange("p (r i) j -> p r j i", i=4),
+                in_=act_rows[s, h][:].rearrange("p j (r i) -> p r j i", i=4),
+            )
 
         def quantize_act(s, h):
             act_codes[s, h] = tile("act_codes_%s_%d" % (s, h), [P, R], U32)
@@ -165,16 +169,19 @@ def tile_speaker_pooled_mean_deviation_k5_kernel(
         y_rows = [tile("y_rows%d" % e, [P, 4, 512], F32) for e in range(2)]
 
         def squash(acc, e, t, rows):
-            nc.scalar.activation(out=squashed[e][:, t, rows], in_=acc, func=ACT.Tanh, bias=bias_f[:, 4 * e + t : 4 * e + t + 1])
+            nc.scalar.activation(out=squashed[e][:, t, rows], in_=acc, func=ACT.Tanh, bias=vecs[:, t, 32 + e : 33 + e])
 
         def apply_gain(e, t, rows):
             nc.vector.tensor_scalar(
                 out=y_t[e][:, t, rows], in0=squashed[e][:, t, rows],
-                scalar1=gain_f[:, 4 * e + t : 4 * e + t + 1], scalar2=None, op0=ALU.mult,
+                scalar1=vecs[:, t, 34 + e : 35 + e], scalar2=None, op0=ALU.mult,
             )
 
         def group_y(e, rows):
-            nc.vector.tensor_copy(out=y_grouped[e][:, rows, :], in_=y_t[e][:, :, rows].rearrange("p t r -> p r t"))
+            nc.vector.tensor_copy(
+                out=y_grouped[e][:, rows, :].rearrange("p (r i) t -> p r t i", i=4),
+                in_=y_t[e][:, :, rows].rearrange("p t (r i) -> p r t i", i=4),
+            )
 
         def quantize_y(e, rows):
             quantize(y_codes[e][:, rows], y_plane[:, e, rows], y_grouped[e][:, rows, :].rearrange("p r t -> p (r t)"))
@@ -199,25 +206,21 @@ def tile_speaker_pooled_mean_deviation_k5_kernel(
             dst = out_1[e].rearrange("p m t -> p (m t)").bitcast(I32)
             queue.dma_start(out=dst[:, rows], in_=y_codes[e][:, rows].bitcast(I32))
 
-        vec_rows = tile("vec_rows", [8, 256], BF16)
-        vec_f = tile("vec_f", [P, 256], F32)
-        offsets = tile("offsets", [P, 2, 8], F32)
-        bias_b = tile("bias_b", [P, 2, 4], BF16)
-        gain_b = tile("gain_b", [P, 2, 4], BF16)
-        bias_f = tile("bias_f", [P, 8], F32)
-        gain_f = tile("gain_f", [P, 8], F32)
+        vec_rows = tile("vec_rows", [36, 512], BF16)
+        vec_f = tile("vec_f", [P, 4, P], F32)
+        vecs = tile("vecs", [P, 4, 36], F32)
         ident = tile("ident", [P, P], F32)
         warm = tile("warm", [P, 8], F32)
 
+        make_identity(nc, ident[:])
+        for row, vec in ((2, var_offset), (0, rec_mean), (32, bias), (34, gain)):
+            nc.gpsimd.dma_start(out=vec_rows[row : row + 2, :], in_=vec.rearrange("(h n) -> h n", h=2))
         nc.vector.memset(attn_plane[:].bitcast(I32), 0)
         nc.vector.memset(plane_raw["dev"][:].bitcast(I32), 0)
         nc.vector.memset(warm[:, 0:1], 1.0)
+        nc.vector.memset(vec_f[:], 0.0)
         nc.vector.memset(plane_raw["mean"][:].bitcast(I32), 0)
-        nc.scalar.dma_start(out=vec_rows[4:8, :].rearrange("j (q c) -> j q c", c=4), in_=var_offset.rearrange("(q j c) -> j q c", j=4, c=4))
-        nc.scalar.dma_start(out=vec_rows[0:4, :].rearrange("j (q c) -> j q c", c=4), in_=rec_mean.rearrange("(q j c) -> j q c", j=4, c=4))
         nc.scalar.activation(out=warm[:, 1:2], in_=warm[:, 0:1], func=ACT.Sqrt)
-        nc.gpsimd.memset(vec_f[:], 0.0)
-        make_identity(nc, ident[:])
 
         nc.sync.dma_start(out=attn_first[:].bitcast(I32), in_=attn_words[0:1].rearrange("g p n -> p g n").bitcast(I32))
         load_words("dev", 0, 0, 1)
@@ -230,15 +233,11 @@ def tile_speaker_pooled_mean_deviation_k5_kernel(
         load_w("dev", 1, 0, 1)
         load_plane(plane_raw["mean"], frame_scales)
         load_words("mean", 0, 0, 4)
-        load_w("mean", 0, 0, 1)
+        load_w("mean", 0, 0, 2)
         load_words("mean", 1, 0, 4)
-        load_w("mean", 1, 0, 1)
-        nc.sync.dma_start(out=bias_b[:], in_=bias.rearrange("(e p t) -> p e t", e=2, t=4))
-        nc.sync.dma_start(out=gain_b[:], in_=gain.rearrange("(e p t) -> p e t", e=2, t=4))
+        load_w("mean", 1, 0, 2)
         load_w("dev", 0, 1, 2)
         load_w("dev", 1, 1, 2)
-        load_w("mean", 0, 1, 2)
-        load_w("mean", 1, 1, 2)
 
         order_words("dev", 0, 0, 1)
         order_plane("dev", 0, 1)
@@ -246,15 +245,19 @@ def tile_speaker_pooled_mean_deviation_k5_kernel(
             pool_pass("dev", 0, j, 0)
         order_plane("dev", 1, 4)
         order_words("dev", 0, 1, 4)
-        nc.vector.tensor_copy(out=vec_f[0:8, :], in_=vec_rows[:])
-        for j in range(4):
-            pool_pass("dev", 0, j, 1)
-        for h in range(2):
-            nc.tensor.transpose(bank[7][:, P * h : P * (h + 1)], vec_f[:, P * h : P * (h + 1)], ident[:])
-        nc.vector.tensor_copy(out=offsets[:], in_=bank[7][:, 0:256].rearrange("p (h v) -> p h v", h=2)[:, :, 0:8])
-        for g in range(2, 4):
+        nc.vector.tensor_copy(
+            out=vec_f[0:4, :, :].rearrange("v j (q c) -> v j q c", c=4),
+            in_=vec_rows[0:4, :].rearrange("v (q j c) -> v j q c", j=4, c=4),
+        )
+        nc.vector.tensor_copy(out=vec_f[32:36, :, :], in_=vec_rows[32:36, :].rearrange("v (m t) -> v t m", t=4))
+        for g in range(1, 3):
             for j in range(4):
                 pool_pass("dev", 0, j, g)
+        for j in range(4):
+            nc.tensor.transpose(bank[7][:, P * j : P * (j + 1)], vec_f[:, j, :], ident[:])
+        nc.vector.tensor_copy(out=vecs[:], in_=bank[7][:].rearrange("p (j v) -> p j v", j=4)[:, :, 0:36])
+        for j in range(4):
+            pool_pass("dev", 0, j, 3)
         group_w("scalar", "dev", 0, 0)
         order_words("dev", 1, 0, 4)
         for j in range(4):
@@ -274,31 +277,29 @@ def tile_speaker_pooled_mean_deviation_k5_kernel(
             pool_group("mean", 0, j)
         order_words("mean", 1, 0, 4)
         quantize_act("dev", 0)
-        group_w("vector", "mean", 1, 0)
+        group_w("vector", "mean", 0, 1)
         quantize_w("mean", 0, 0)
         group_act("dev", 1)
-        quantize_w("mean", 1, 0)
-        group_w("scalar", "dev", 0, 1)
+        quantize_w("mean", 0, 1)
+        group_w("scalar", "mean", 1, 0)
         for j in range(4):
             finish_pool("mean", 0, j)
         for j in range(4):
             pool_group("mean", 1, j)
-        nc.vector.tensor_copy(out=bias_f[:], in_=bias_b[:].rearrange("p e t -> p (e t)"))
-        nc.vector.tensor_copy(out=gain_f[:], in_=gain_b[:].rearrange("p e t -> p (e t)"))
-        group_w("vector", "dev", 1, 1)
+        group_w("vector", "mean", 1, 1)
         quantize_act("dev", 1)
-        group_w("vector", "mean", 0, 1)
-        quantize_w("dev", 0, 1)
+        group_w("vector", "dev", 0, 1)
+        quantize_w("mean", 1, 0)
         group_act("mean", 0)
-        quantize_w("dev", 1, 1)
+        quantize_w("mean", 1, 1)
         quantize_act("mean", 0)
         for j in range(4):
             finish_pool("mean", 1, j)
-        group_w("vector", "mean", 1, 1)
+        group_w("vector", "dev", 1, 1)
         group_act("mean", 1)
-        quantize_w("mean", 0, 1)
+        quantize_w("dev", 0, 1)
         quantize_act("mean", 1)
-        quantize_w("mean", 1, 1)
+        quantize_w("dev", 1, 1)
 
         whole = slice(0, R)
         halves = [slice(0, 256), slice(256, 512)]

@@ -17,6 +17,7 @@ ACT = mybir.ActivationFunctionType
 ALU = mybir.AluOpType
 
 P = 128
+UNITS = [(0, "a"), (0, "b"), (1, "a"), (1, "b")]
 G = T // 512
 
 
@@ -30,13 +31,12 @@ def tile_speaker_pooled_mean_deviation_k5_kernel(
         psum = ctx.enter_context(tc.psum_pool(name="psum", bufs=1))
         ctx.enter_context(tc.manual_schedule())
 
-        def tile(name, shape, dtype, tag="", bufs=None):
-            return sb.tile(shape, dtype, name=name, tag=tag, bufs=bufs, align_bytes=64)
+        def tile(name, shape, dtype):
+            return sb.tile(shape, dtype, name=name, align_bytes=64)
 
         bank = [psum.tile([P, 512], F32, name="bank%d" % i) for i in range(8)]
 
-        attn_first = tile("attn_first", [P, 1, 1024], U8)
-        attn_rest = tile("attn_rest", [P, 3, 1024], U8)
+        attn_codes = {}
         attn_plane = tile("attn_plane", [P, G, 512], U8)
         words_in = {"dev": square_words, "mean": frame_words}
         scales_in = {"dev": square_scales, "mean": frame_scales}
@@ -54,29 +54,31 @@ def tile_speaker_pooled_mean_deviation_k5_kernel(
         act_codes = {}
         act_plane = {}
 
-        def attn(g):
-            src = attn_first[:, 0, :] if g == 0 else attn_rest[:, g - 1, :]
-            return src.bitcast(FP4X4)
-
-        def load_plane(dst, src):
-            rows = src.rearrange("g (q r) n -> r q g n", r=4)
-            for r in range(4):
-                nc.sync.dma_start(out=dst[r:P:32, :, :].bitcast(I32), in_=rows[r].bitcast(I32))
-
-        def load_words(s, h, g0, g1):
-            raw = tile("words_raw_%s_%d_%d" % (s, h, g0), [P, g1 - g0, 1024], U8)
-            words_raw[s, h, g0] = raw
-            src = words_in[s][g0:g1, :, 1024 * h : 1024 * (h + 1)].rearrange("g p n -> p g n")
-            nc.sync.dma_start(out=raw[:].bitcast(I32), in_=src.bitcast(I32))
-
-        def order_words(s, h, g0, g1):
-            dst = tile("words_%s_%d_%d" % (s, h, g0), [P, 4, g1 - g0, 256], U8)
+        def load_attn(g0, g1):
+            dst = tile("attn_codes_%d" % g0, [P, g1 - g0, 1024], U8)
             for g in range(g0, g1):
-                for j in range(4):
-                    words[s, h, j, g] = dst[:, j, g - g0, :]
+                attn_codes[g] = dst[:, g - g0, :]
+            nc.sync.dma_start(out=dst[:].bitcast(I32), in_=attn_words[g0:g1].rearrange("g p n -> p g n").bitcast(I32))
+
+        def load_plane(queue, dst, src, g0, g1):
+            rows = src[g0:g1].rearrange("g (q r) n -> r q g n", r=4)
+            for r in range(4):
+                queue.dma_start(out=dst[r:P:32, g0:g1, :].bitcast(I32), in_=rows[r].bitcast(I32))
+
+        def load_words(s, g0, g1):
+            raw = tile("words_raw_%s_%d" % (s, g0), [P, g1 - g0, 2048], U8)
+            words_raw[s, g0] = raw
+            nc.sync.dma_start(out=raw[:].bitcast(I32), in_=words_in[s][g0:g1].rearrange("g p n -> p g n").bitcast(I32))
+
+        def order_words(s, g0, g1):
+            dst = tile("words_%s_%d" % (s, g0), [P, 4, g1 - g0, 512], U8)
+            for g in range(g0, g1):
+                for h in range(2):
+                    for j in range(4):
+                        words[s, h, j, g] = dst[:, j, g - g0, 256 * h : 256 * (h + 1)]
             nc.vector.tensor_copy(
                 out=dst[:].bitcast(I32).rearrange("p j g (q w) -> p j (g q) w", w=2),
-                in_=words_raw[s, h, g0][:].bitcast(I32).rearrange("p g (q j w) -> p j (g q) w", j=4, w=2),
+                in_=words_raw[s, g0][:].bitcast(I32).rearrange("p g (q j w) -> p j (g q) w", j=4, w=2),
             )
 
         def order_plane(s, g0, g1):
@@ -98,11 +100,11 @@ def tile_speaker_pooled_mean_deviation_k5_kernel(
             for c in range(4):
                 nc.sync.dma_start(out=raw[c:P:4, :, :], in_=rows[c])
 
-        def group_w(engine, s, h, e):
-            dst = tile("w_grouped_%s_%d_%d" % (s, h, e), [P, 4, P, 4], BF16, "w_grouped", 4)
-            w_grouped[s, h, e] = dst
-            src = w_raw[s, h, e].rearrange("p j (m a t) -> p m t a j", a=2, t=4)
-            out = dst[:].rearrange("p t (m a) j -> p m t a j", a=2)
+        def group_w(engine, s, h, e, t0=0, t1=4):
+            if (s, h, e) not in w_grouped:
+                w_grouped[s, h, e] = tile("w_grouped_%s_%d_%d" % (s, h, e), [P, 4, P, 4], BF16)
+            src = w_raw[s, h, e].rearrange("p j (m a t) -> p m t a j", a=2, t=4)[:, :, t0:t1]
+            out = w_grouped[s, h, e][:].rearrange("p t (m a) j -> p m t a j", a=2)[:, :, t0:t1]
             if engine == "vector":
                 nc.vector.tensor_copy(out=out, in_=src)
             else:
@@ -116,83 +118,95 @@ def tile_speaker_pooled_mean_deviation_k5_kernel(
             w_plane[s, h, e] = tile("w_plane_%s_%d_%d" % (s, h, e), [P, 512], U8)
             quantize(w_codes[s, h, e][:], w_plane[s, h, e][:], w_grouped[s, h, e][:].rearrange("p t m j -> p (t m j)"))
 
-        def pool_pass(s, h, j, g):
+        spans = {"all": slice(0, R), "a": slice(0, 256), "b": slice(256, 512), "c": slice(256, 384), "d": slice(384, 512)}
+
+        def pool_pass(s, h, j, g, u):
+            rows = spans[u]
             nc.tensor.matmul_mx(
-                out=bank[4 * h + j][:],
+                out=bank[4 * h + j][:, rows],
                 lhsT=words[s, h, j, g].bitcast(FP4X4), lhsT_scale=plane[s, h, j, g],
-                rhs=attn(g), rhs_scale=attn_plane[:, g, :],
+                rhs=attn_codes[g][:, 2 * rows.start : 2 * rows.stop].bitcast(FP4X4), rhs_scale=attn_plane[:, g, rows],
                 start=(g == 0), stop=(g == G - 1),
             )
 
-        def pool_group(s, h, j):
-            for g in range(G):
-                pool_pass(s, h, j, g)
+        for s, us in (("dev", ["all"]), ("mean", ["a", "b"])):
+            for h in range(2):
+                act_codes[s, h] = tile("act_codes_%s_%d" % (s, h), [P, R], U32)
+                act_plane[s, h] = tile("act_plane_%s_%d" % (s, h), [P, R], U8)
+                for u in us:
+                    n = spans[u].stop - spans[u].start
+                    act_rows[s, h, u] = tile("act_rows_%s_%d_%s" % (s, h, u), [P, 4, n], BF16)
+                    act_grouped[s, h, u] = tile("act_grouped_%s_%d_%s" % (s, h, u), [P, n, 4], BF16)
 
-        def finish_pool(s, h, j):
-            if j == 0:
-                act_rows[s, h] = tile("act_rows_%s_%d" % (s, h), [P, 4, R], BF16, "act_rows", 2)
+        def finish_pool(engine, s, h, j, u):
             col = (2 if s == "dev" else 0) + h
-            nc.scalar.activation(
-                out=act_rows[s, h][:, j, :], in_=bank[4 * h + j][:],
-                func=ACT.Sqrt if s == "dev" else ACT.Identity, bias=vecs[:, j, col : col + 1],
-            )
+            out, acc, offset = act_rows[s, h, u][:, j, :], bank[4 * h + j][:, spans[u]], vecs[:, j, col : col + 1]
+            if engine == "vector":
+                nc.vector.tensor_scalar(out=out, in0=acc, scalar1=offset, scalar2=None, op0=ALU.add)
+            else:
+                nc.scalar.activation(out=out, in_=acc, func=ACT.Sqrt if s == "dev" else ACT.Identity, bias=offset)
 
-        def group_act(s, h):
-            act_grouped[s, h] = tile("act_grouped_%s_%d" % (s, h), [P, R, 4], BF16, "act_grouped", 2)
-            nc.vector.tensor_copy(
-                out=act_grouped[s, h][:].rearrange("p (r i) j -> p r j i", i=4),
-                in_=act_rows[s, h][:].rearrange("p j (r i) -> p r j i", i=4),
-            )
+        def interleave(engine, out, rows):
+            out = out.rearrange("p (r i) j -> p r j i", i=4)
+            rows = rows.rearrange("p j (r i) -> p r j i", i=4)
+            if engine == "vector":
+                nc.vector.tensor_copy(out=out, in_=rows)
+            else:
+                nc.scalar.copy(out=out, in_=rows)
 
-        def quantize_act(s, h):
-            act_codes[s, h] = tile("act_codes_%s_%d" % (s, h), [P, R], U32)
-            act_plane[s, h] = tile("act_plane_%s_%d" % (s, h), [P, R], U8)
-            quantize(act_codes[s, h][:], act_plane[s, h][:], act_grouped[s, h][:].rearrange("p r j -> p (r j)"))
+        def group_act(engine, s, h, u, part=None):
+            rows = spans[part] if part else slice(0, 256)
+            interleave(engine, act_grouped[s, h, u][:, rows, :], act_rows[s, h, u][:, :, rows])
+
+        def quantize_act(s, h, u):
+            quantize(act_codes[s, h][:, spans[u]], act_plane[s, h][:, spans[u]], act_grouped[s, h, u][:].rearrange("p r j -> p (r j)"))
 
         passes = [("dev", 0), ("dev", 1), ("mean", 0), ("mean", 1)]
 
-        def embed_pass(acc, e, t, rows, i):
-            s, h = passes[i]
+        def embed(e, u, t):
+            rows = spans[u]
             cols = slice(P * t, P * (t + 1))
-            nc.tensor.matmul_mx(
-                out=acc,
-                lhsT=w_codes[s, h, e][:, cols].bitcast(FP8X4), lhsT_scale=w_plane[s, h, e][:, cols],
-                rhs=act_codes[s, h][:, rows].bitcast(FP8X4), rhs_scale=act_plane[s, h][:, rows],
-                start=(i == 0), stop=(i == 3),
-            )
+            for i, (s, h) in enumerate(passes):
+                nc.tensor.matmul_mx(
+                    out=bank[t][:, rows],
+                    lhsT=w_codes[s, h, e][:, cols].bitcast(FP8X4), lhsT_scale=w_plane[s, h, e][:, cols],
+                    rhs=act_codes[s, h][:, rows].bitcast(FP8X4), rhs_scale=act_plane[s, h][:, rows],
+                    start=(i == 0), stop=(i == 3),
+                )
 
-        squashed = [tile("squashed%d" % e, [P, 4, R], F32) for e in range(2)]
-        y_t = [tile("y_t%d" % e, [P, 4, R], F32) for e in range(2)]
-        y_grouped = [tile("y_grouped%d" % e, [P, R, 4], BF16) for e in range(2)]
+        units = UNITS
+        y_t = {k: tile("y_t%d%s" % k, [P, 4, spans[k[1]].stop - spans[k[1]].start], F32) for k in units}
+        y_grouped = {k: tile("y_grouped%d%s" % k, [P, spans[k[1]].stop - spans[k[1]].start, 4], BF16) for k in units}
         y_codes = [tile("y_codes%d" % e, [P, R], U32) for e in range(2)]
         y_plane = tile("y_plane", [P, 2, R], U8)
         y_rows = [tile("y_rows%d" % e, [P, 4, 512], F32) for e in range(2)]
 
-        def squash(acc, e, t, rows):
-            nc.scalar.activation(out=squashed[e][:, t, rows], in_=acc, func=ACT.Tanh, bias=vecs[:, t, 32 + e : 33 + e])
+        def squash(e, u, t):
+            nc.scalar.activation(out=y_t[e, u][:, t, :], in_=bank[t][:, spans[u]], func=ACT.Tanh, bias=vecs[:, t, 32 + e : 33 + e])
 
-        def apply_gain(e, t, rows):
-            nc.vector.tensor_scalar(
-                out=y_t[e][:, t, rows], in0=squashed[e][:, t, rows],
-                scalar1=vecs[:, t, 34 + e : 35 + e], scalar2=None, op0=ALU.mult,
-            )
+        def apply_gain(engine, e, u, t):
+            if engine == "vector":
+                nc.vector.tensor_scalar(
+                    out=y_t[e, u][:, t, :], in0=y_t[e, u][:, t, :],
+                    scalar1=vecs[:, t, 34 + e : 35 + e], scalar2=None, op0=ALU.mult,
+                )
+            else:
+                nc.scalar.activation(out=y_t[e, u][:, t, :], in_=y_t[e, u][:, t, :], func=ACT.Copy, scale=vecs[:, t, 34 + e : 35 + e])
 
-        def group_y(e, rows):
-            nc.vector.tensor_copy(
-                out=y_grouped[e][:, rows, :].rearrange("p (r i) t -> p r t i", i=4),
-                in_=y_t[e][:, :, rows].rearrange("p t (r i) -> p r t i", i=4),
-            )
+        def group_y(e, u):
+            interleave("vector", y_grouped[e, u][:], y_t[e, u][:])
 
-        def quantize_y(e, rows):
-            quantize(y_codes[e][:, rows], y_plane[:, e, rows], y_grouped[e][:, rows, :].rearrange("p r t -> p (r t)"))
+        def quantize_y(e, u):
+            quantize(y_codes[e][:, spans[u]], y_plane[:, e, spans[u]], y_grouped[e, u][:].rearrange("p r t -> p (r t)"))
 
-        def turn(b, e, rb):
+        def turn(e, u, rb):
             for t in range(4):
-                nc.tensor.transpose(bank[b][:, P * t : P * (t + 1)], y_t[e][:, t, P * rb : P * (rb + 1)], ident[:])
+                src = y_t[e, u][:, t, P * rb - spans[u].start : P * (rb + 1) - spans[u].start]
+                nc.tensor.transpose(bank[4 + rb][:, P * t : P * (t + 1)], src, ident[:])
 
-        def unload(engine, b, e, rb):
+        def unload(engine, e, rb):
             dst = y_rows[e][:, rb, :].rearrange("p (m t) -> p m t", t=4)
-            src = bank[b][:].rearrange("p (t m) -> p m t", t=4)
+            src = bank[4 + rb][:].rearrange("p (t m) -> p m t", t=4)
             if engine == "vector":
                 nc.vector.tensor_copy(out=dst, in_=src)
             else:
@@ -202,9 +216,35 @@ def tile_speaker_pooled_mean_deviation_k5_kernel(
             dst = out_0[P * rb0 : P * rb1, 512 * e : 512 * (e + 1)].rearrange("(b p) n -> p b n", p=P)
             queue.dma_start(out=dst, in_=y_rows[e][:, rb0:rb1, :])
 
-        def store_codes(queue, e, rows):
+        def store_codes(queue, e, u):
             dst = out_1[e].rearrange("p m t -> p (m t)").bitcast(I32)
-            queue.dma_start(out=dst[:, rows], in_=y_codes[e][:, rows].bitcast(I32))
+            queue.dma_start(out=dst[:, spans[u]], in_=y_codes[e][:, spans[u]].bitcast(I32))
+
+        def vec_turn():
+            for j in range(4):
+                nc.tensor.transpose(bank[7][:, P * j : P * (j + 1)], vec_f[:, j, :], ident[:])
+
+        def vec_unload():
+            nc.vector.tensor_copy(out=vecs[:], in_=bank[7][:].rearrange("p (j v) -> p j v", j=4)[:, :, 0:36])
+
+        def pool_run(s, u, gs, groups):
+            for h, j in groups:
+                for g in gs:
+                    pool_pass(s, h, j, g, u)
+
+        groups = [(h, j) for h in range(2) for j in range(4)]
+
+        def store_plane(queues):
+            plane_rows = out_2.rearrange("g (q r) m -> r q g m", r=4)
+            for r in range(4):
+                queues[r].dma_start(out=plane_rows[r].bitcast(I32), in_=y_plane[r:P:32, :, :].bitcast(I32))
+
+        def vec_order():
+            nc.vector.tensor_copy(
+                out=vec_f[0:4, :, :].rearrange("v j (q c) -> v j q c", c=4),
+                in_=vec_rows[0:4, :].rearrange("v (q j c) -> v j q c", j=4, c=4),
+            )
+            nc.vector.tensor_copy(out=vec_f[32:36, :, :], in_=vec_rows[32:36, :].rearrange("v (m t) -> v t m", t=4))
 
         vec_rows = tile("vec_rows", [36, 512], BF16)
         vec_f = tile("vec_f", [P, 4, P], F32)
@@ -214,146 +254,209 @@ def tile_speaker_pooled_mean_deviation_k5_kernel(
 
         make_identity(nc, ident[:])
         for row, vec in ((2, var_offset), (0, rec_mean), (32, bias), (34, gain)):
-            nc.gpsimd.dma_start(out=vec_rows[row : row + 2, :], in_=vec.rearrange("(h n) -> h n", h=2))
-        nc.vector.memset(attn_plane[:].bitcast(I32), 0)
+            nc.scalar.dma_start(out=vec_rows[row : row + 2, :], in_=vec.rearrange("(h n) -> h n", h=2))
         nc.vector.memset(plane_raw["dev"][:].bitcast(I32), 0)
+        nc.vector.memset(attn_plane[:].bitcast(I32), 0)
         nc.vector.memset(warm[:, 0:1], 1.0)
         nc.vector.memset(vec_f[:], 0.0)
         nc.vector.memset(plane_raw["mean"][:].bitcast(I32), 0)
         nc.scalar.activation(out=warm[:, 1:2], in_=warm[:, 0:1], func=ACT.Sqrt)
 
-        nc.sync.dma_start(out=attn_first[:].bitcast(I32), in_=attn_words[0:1].rearrange("g p n -> p g n").bitcast(I32))
-        load_words("dev", 0, 0, 1)
-        load_plane(attn_plane, attn_scales)
-        load_plane(plane_raw["dev"], square_scales)
-        nc.sync.dma_start(out=attn_rest[:].bitcast(I32), in_=attn_words[1:4].rearrange("g p n -> p g n").bitcast(I32))
-        load_words("dev", 0, 1, 4)
-        load_w("dev", 0, 0, 1)
-        load_words("dev", 1, 0, 4)
-        load_w("dev", 1, 0, 1)
-        load_plane(plane_raw["mean"], frame_scales)
-        load_words("mean", 0, 0, 4)
+        vec_order()
+        vec_turn()
+        load_words("dev", 2, 4)
+        load_words("dev", 0, 1)
+        vec_unload()
+        load_plane(nc.sync, plane_raw["dev"], square_scales, 0, 4)
+        load_plane(nc.sync, attn_plane, attn_scales, 0, 4)
+        load_attn(0, 1)
+        load_words("dev", 1, 2)
+        load_attn(1, 2)
         load_w("mean", 0, 0, 2)
-        load_words("mean", 1, 0, 4)
-        load_w("mean", 1, 0, 2)
-        load_w("dev", 0, 1, 2)
-        load_w("dev", 1, 1, 2)
-
-        order_words("dev", 0, 0, 1)
+        order_words("dev", 0, 1)
         order_plane("dev", 0, 1)
-        for j in range(4):
-            pool_pass("dev", 0, j, 0)
         order_plane("dev", 1, 4)
-        order_words("dev", 0, 1, 4)
-        nc.vector.tensor_copy(
-            out=vec_f[0:4, :, :].rearrange("v j (q c) -> v j q c", c=4),
-            in_=vec_rows[0:4, :].rearrange("v (q j c) -> v j q c", j=4, c=4),
-        )
-        nc.vector.tensor_copy(out=vec_f[32:36, :, :], in_=vec_rows[32:36, :].rearrange("v (m t) -> v t m", t=4))
-        for g in range(1, 3):
-            for j in range(4):
-                pool_pass("dev", 0, j, g)
-        for j in range(4):
-            nc.tensor.transpose(bank[7][:, P * j : P * (j + 1)], vec_f[:, j, :], ident[:])
-        nc.vector.tensor_copy(out=vecs[:], in_=bank[7][:].rearrange("p (j v) -> p j v", j=4)[:, :, 0:36])
-        for j in range(4):
-            pool_pass("dev", 0, j, 3)
-        group_w("scalar", "dev", 0, 0)
-        order_words("dev", 1, 0, 4)
-        for j in range(4):
-            finish_pool("dev", 0, j)
-        for j in range(4):
-            pool_group("dev", 1, j)
-        group_w("vector", "dev", 1, 0)
-        quantize_w("dev", 0, 0)
+        order_words("dev", 2, 4)
+        load_attn(2, 4)
+        group_w("scalar", "mean", 0, 0, 0, 2)
+        pool_run("dev", "all", [0], groups)
+        order_words("dev", 1, 2)
+        load_plane(nc.gpsimd, plane_raw["mean"], frame_scales, 0, 4)
+        pool_run("dev", "all", [1], groups)
+        load_words("mean", 2, 4)
+        pool_run("dev", "all", [2, 3], groups[0:1])
         order_plane("mean", 0, 4)
-        quantize_w("dev", 1, 0)
-        order_words("mean", 0, 0, 4)
-        group_act("dev", 0)
-        group_w("scalar", "mean", 0, 0)
-        for j in range(4):
-            finish_pool("dev", 1, j)
-        for j in range(4):
-            pool_group("mean", 0, j)
-        order_words("mean", 1, 0, 4)
-        quantize_act("dev", 0)
-        group_w("vector", "mean", 0, 1)
-        quantize_w("mean", 0, 0)
-        group_act("dev", 1)
+        group_w("vector", "mean", 0, 0, 2, 4)
+        load_words("mean", 0, 2)
+        group_w("vector", "mean", 0, 1, 0, 4)
+        load_w("mean", 1, 0, 2)
+        finish_pool("scalar", "dev", 0, 0, "all")
+        pool_run("dev", "all", [2, 3], groups[1:2])
+        pool_run("dev", "all", [2, 3], groups[2:3])
+        order_words("mean", 2, 4)
+        pool_run("dev", "all", [2, 3], groups[3:4])
+        load_w("dev", 0, 0, 2)
         quantize_w("mean", 0, 1)
-        group_w("scalar", "mean", 1, 0)
-        for j in range(4):
-            finish_pool("mean", 0, j)
-        for j in range(4):
-            pool_group("mean", 1, j)
-        group_w("vector", "mean", 1, 1)
-        quantize_act("dev", 1)
-        group_w("vector", "dev", 0, 1)
+        pool_run("dev", "all", [2, 3], groups[4:5])
+        order_words("mean", 0, 2)
+        pool_run("dev", "all", [2, 3], groups[5:6])
+        pool_run("dev", "all", [2, 3], groups[6:7])
+        finish_pool("scalar", "dev", 0, 1, "all")
+        quantize_w("mean", 0, 0)
+        finish_pool("scalar", "dev", 0, 2, "all")
+        finish_pool("scalar", "dev", 0, 3, "all")
+        finish_pool("scalar", "dev", 1, 0, "all")
+        finish_pool("scalar", "dev", 1, 1, "all")
+        group_act("vector", "dev", 0, "all", "all")
+        pool_run("dev", "all", [2, 3], groups[7:8])
+        finish_pool("scalar", "dev", 1, 2, "all")
+        finish_pool("scalar", "dev", 1, 3, "all")
+        group_w("scalar", "mean", 1, 0, 0, 2)
+        group_w("vector", "mean", 1, 0, 2, 4)
+        pool_run("mean", "a", [0], groups)
+        pool_run("mean", "a", [1], groups)
+        pool_run("mean", "a", [2, 3], groups[0:1])
+        quantize_act("dev", 0, "all")
+        pool_run("mean", "a", [2, 3], groups[1:2])
+        group_w("vector", "mean", 1, 1, 0, 2)
+        group_act("vector", "dev", 1, "all", "all")
+        pool_run("mean", "a", [2, 3], groups[2:3])
+        pool_run("mean", "a", [2, 3], groups[3:4])
+        pool_run("mean", "a", [2, 3], groups[4:5])
+        group_w("scalar", "dev", 0, 1, 0, 2)
+        finish_pool("scalar", "mean", 0, 0, "a")
+        finish_pool("scalar", "mean", 0, 1, "a")
+        pool_run("mean", "a", [2, 3], groups[5:6])
+        pool_run("mean", "a", [2, 3], groups[6:7])
+        finish_pool("scalar", "mean", 0, 2, "a")
+        finish_pool("scalar", "mean", 0, 3, "a")
+        finish_pool("scalar", "mean", 1, 0, "a")
+        finish_pool("scalar", "mean", 1, 1, "a")
+        pool_run("mean", "a", [2, 3], groups[7:8])
+        pool_run("mean", "b", [0, 1, 2, 3], groups[0:1])
+        finish_pool("scalar", "mean", 1, 2, "a")
+        finish_pool("scalar", "mean", 1, 3, "a")
+        group_w("vector", "dev", 0, 0, 0, 2)
+        quantize_act("dev", 1, "all")
+        group_w("vector", "dev", 0, 0, 2, 4)
+        pool_run("mean", "b", [0, 1, 2, 3], groups[1:2])
+        load_w("dev", 1, 0, 2)
+        group_w("scalar", "dev", 1, 0, 0, 2)
+        finish_pool("scalar", "mean", 0, 0, "b")
+        finish_pool("scalar", "mean", 0, 1, "b")
+        pool_run("mean", "b", [0, 1, 2, 3], groups[2:3])
+        pool_run("mean", "b", [0, 1, 2, 3], groups[3:4])
+        finish_pool("scalar", "mean", 0, 2, "b")
+        pool_run("mean", "b", [0, 1, 2, 3], groups[4:5])
+        group_act("vector", "mean", 0, "a")
+        pool_run("mean", "b", [0, 1, 2, 3], groups[5:6])
+        group_w("vector", "dev", 1, 0, 2, 4)
+        quantize_w("dev", 0, 0)
+        group_act("vector", "mean", 1, "a")
+        finish_pool("scalar", "mean", 0, 3, "b")
+        quantize_act("mean", 0, "a")
+        finish_pool("scalar", "mean", 1, 0, "b")
+        quantize_w("dev", 1, 0)
+        finish_pool("scalar", "mean", 1, 1, "b")
+        quantize_act("mean", 1, "a")
+        pool_run("mean", "b", [0, 1, 2, 3], groups[6:7])
+        pool_run("mean", "b", [0, 1, 2, 3], groups[7:8])
         quantize_w("mean", 1, 0)
-        group_act("mean", 0)
-        quantize_w("mean", 1, 1)
-        quantize_act("mean", 0)
-        for j in range(4):
-            finish_pool("mean", 1, j)
-        group_w("vector", "dev", 1, 1)
-        group_act("mean", 1)
+        finish_pool("scalar", "mean", 1, 2, "b")
+        embed(0, "a", 0)
+        group_act("vector", "mean", 0, "b")
+        embed(0, "a", 1)
+        embed(0, "a", 2)
+        finish_pool("scalar", "mean", 1, 3, "b")
+        squash(0, "a", 0)
+        group_w("vector", "dev", 0, 1, 2, 4)
+        squash(0, "a", 1)
+        group_act("vector", "mean", 1, "b")
+        squash(0, "a", 2)
+        quantize_act("mean", 0, "b")
+        apply_gain("scalar", 0, "a", 0)
+        quantize_act("mean", 1, "b")
+        embed(0, "a", 3)
+        squash(0, "a", 3)
+        group_w("vector", "dev", 1, 1, 0, 2)
+        apply_gain("vector", 0, "a", 1)
+        apply_gain("scalar", 0, "a", 2)
+        embed(0, "b", 0)
+        group_w("vector", "dev", 1, 1, 2, 4)
+        apply_gain("vector", 0, "a", 3)
         quantize_w("dev", 0, 1)
-        quantize_act("mean", 1)
+        group_w("scalar", "mean", 1, 1, 2, 4)
+        squash(0, "b", 0)
+        embed(0, "b", 1)
+        squash(0, "b", 1)
         quantize_w("dev", 1, 1)
-
-        whole = slice(0, R)
-        halves = [slice(0, 256), slice(256, 512)]
-        for i in range(4):
-            for t in range(4):
-                embed_pass(bank[t][:], 0, t, whole, i)
-        for t in range(4):
-            squash(bank[t][:], 0, t, whole)
-            apply_gain(0, t, whole)
-
-        def half_acc(u, t):
-            return bank[4 + 2 * u + t // 2][:, 256 * (t % 2) : 256 * (t % 2 + 1)]
-
-        def embed_half(u):
-            for t in range(4):
-                for i in range(4):
-                    embed_pass(half_acc(u, t), 1, t, halves[u], i)
-
-        embed_half(0)
-        for rb in range(4):
-            turn(rb, 0, rb)
-        group_y(0, whole)
-        for t in range(4):
-            squash(half_acc(0, t), 1, t, halves[0])
-            apply_gain(1, t, halves[0])
-        quantize_y(0, whole)
-        store_codes(nc.sync, 0, whole)
-        embed_half(1)
-        unload("scalar", 0, 0, 0)
-        unload("vector", 1, 0, 1)
-        unload("scalar", 2, 0, 2)
-        store_rows(nc.sync, 0, 0, 2)
-        group_y(1, halves[0])
-        unload("scalar", 3, 0, 3)
-        store_rows(nc.sync, 0, 2, 4)
-        quantize_y(1, halves[0])
-        store_codes(nc.sync, 1, halves[0])
-        for t in range(4):
-            squash(half_acc(1, t), 1, t, halves[1])
-            apply_gain(1, t, halves[1])
-        turn(0, 1, 0)
-        turn(1, 1, 1)
-        turn(2, 1, 2)
-        turn(3, 1, 3)
-        unload("scalar", 0, 1, 0)
-        group_y(1, halves[1])
-        unload("scalar", 1, 1, 1)
-        store_rows(nc.sync, 1, 0, 2)
-        quantize_y(1, halves[1])
-        unload("scalar", 2, 1, 2)
-        store_codes(nc.sync, 1, halves[1])
-        plane_rows = out_2.rearrange("g (q r) m -> r q g m", r=4)
-        for r in range(4):
-            nc.sync.dma_start(out=plane_rows[r].bitcast(I32), in_=y_plane[r:P:32, :, :].bitcast(I32))
-        unload("vector", 3, 1, 3)
+        embed(0, "b", 2)
+        turn(0, "a", 0)
+        squash(0, "b", 2)
+        quantize_w("mean", 1, 1)
+        turn(0, "a", 1)
+        group_y(0, "a")
+        embed(0, "b", 3)
+        apply_gain("vector", 0, "b", 0)
+        unload("scalar", 0, 0)
+        embed(1, "a", 0)
+        squash(0, "b", 3)
+        store_rows(nc.sync, 0, 0, 1)
+        quantize_y(0, "a")
+        apply_gain("vector", 0, "b", 1)
+        apply_gain("vector", 0, "b", 2)
+        store_codes(nc.sync, 0, "a")
+        squash(1, "a", 0)
+        embed(1, "a", 1)
+        apply_gain("vector", 0, "b", 3)
+        embed(1, "a", 2)
+        embed(1, "a", 3)
+        apply_gain("vector", 1, "a", 0)
+        unload("scalar", 0, 1)
+        squash(1, "a", 1)
+        group_y(0, "b")
+        store_rows(nc.sync, 0, 1, 2)
+        turn(0, "b", 2)
+        squash(1, "a", 2)
+        apply_gain("vector", 1, "a", 1)
+        squash(1, "a", 3)
+        quantize_y(0, "b")
+        unload("scalar", 0, 2)
+        turn(0, "b", 3)
+        embed(1, "b", 0)
+        embed(1, "b", 1)
+        apply_gain("vector", 1, "a", 2)
+        apply_gain("vector", 1, "a", 3)
+        unload("scalar", 0, 3)
+        embed(1, "b", 2)
+        embed(1, "b", 3)
+        store_codes(nc.sync, 0, "b")
+        turn(1, "a", 0)
+        store_rows(nc.sync, 0, 2, 3)
+        group_y(1, "a")
+        squash(1, "b", 0)
+        store_rows(nc.sync, 0, 3, 4)
+        quantize_y(1, "a")
+        turn(1, "a", 1)
+        apply_gain("vector", 1, "b", 0)
+        squash(1, "b", 1)
+        apply_gain("vector", 1, "b", 1)
+        squash(1, "b", 2)
+        apply_gain("vector", 1, "b", 2)
+        store_codes(nc.sync, 1, "a")
+        squash(1, "b", 3)
+        unload("scalar", 1, 0)
+        apply_gain("vector", 1, "b", 3)
+        unload("vector", 1, 1)
+        store_rows(nc.sync, 1, 0, 1)
+        group_y(1, "b")
+        turn(1, "b", 2)
+        store_rows(nc.sync, 1, 1, 2)
+        quantize_y(1, "b")
+        turn(1, "b", 3)
+        unload("scalar", 1, 2)
         store_rows(nc.scalar, 1, 2, 3)
+        store_plane([nc.sync] * 4)
+        unload("scalar", 1, 3)
+        store_codes(nc.sync, 1, "b")
         store_rows(nc.sync, 1, 3, 4)

@@ -17,7 +17,7 @@ ACT = mybir.ActivationFunctionType
 ALU = mybir.AluOpType
 
 P = 128
-UNITS = [(0, "a"), (0, "b"), (1, "a"), (1, "b")]
+UNITS = [(0, "all"), (1, "a"), (1, "b")]
 G = T // 512
 
 
@@ -129,7 +129,7 @@ def tile_speaker_pooled_mean_deviation_k5_kernel(
                 start=(g == 0), stop=(g == G - 1),
             )
 
-        for s, us in (("dev", ["all"]), ("mean", ["a", "b"])):
+        for s, us in (("dev", ["all"]), ("mean", ["all"])):
             for h in range(2):
                 act_codes[s, h] = tile("act_codes_%s_%d" % (s, h), [P, R], U32)
                 act_plane[s, h] = tile("act_plane_%s_%d" % (s, h), [P, R], U8)
@@ -159,14 +159,15 @@ def tile_speaker_pooled_mean_deviation_k5_kernel(
             interleave(engine, act_grouped[s, h, u][:, rows, :], act_rows[s, h, u][:, :, rows])
 
         def quantize_act(s, h, u):
-            quantize(act_codes[s, h][:, spans[u]], act_plane[s, h][:, spans[u]], act_grouped[s, h, u][:].rearrange("p r j -> p (r j)"))
+            quantize(act_codes[s, h][:, spans[u]], act_plane[s, h][:, spans[u]], act_grouped[s, h, "all"][:, spans[u], :].rearrange("p r j -> p (r j)"))
 
         passes = [("dev", 0), ("dev", 1), ("mean", 0), ("mean", 1)]
 
-        def embed(e, u, t):
+        def embed(e, u, t, i0=0, i1=4):
             rows = spans[u]
             cols = slice(P * t, P * (t + 1))
-            for i, (s, h) in enumerate(passes):
+            for i in range(i0, i1):
+                s, h = passes[i]
                 nc.tensor.matmul_mx(
                     out=bank[t][:, rows],
                     lhsT=w_codes[s, h, e][:, cols].bitcast(FP8X4), lhsT_scale=w_plane[s, h, e][:, cols],
@@ -193,11 +194,14 @@ def tile_speaker_pooled_mean_deviation_k5_kernel(
             else:
                 nc.scalar.activation(out=y_t[e, u][:, t, :], in_=y_t[e, u][:, t, :], func=ACT.Copy, scale=vecs[:, t, 34 + e : 35 + e])
 
-        def group_y(e, u):
-            interleave("vector", y_grouped[e, u][:], y_t[e, u][:])
+        def group_y(e, u, part=None):
+            rows = spans[part] if part else slice(0, 256)
+            interleave("vector", y_grouped[e, u][:, rows, :], y_t[e, u][:, :, rows])
 
-        def quantize_y(e, u):
-            quantize(y_codes[e][:, spans[u]], y_plane[:, e, spans[u]], y_grouped[e, u][:].rearrange("p r t -> p (r t)"))
+        def quantize_y(e, u, part=None):
+            rows = spans[part] if part else slice(0, 256)
+            at = spans[part or u]
+            quantize(y_codes[e][:, at], y_plane[:, e, at], y_grouped[e, u][:, rows, :].rearrange("p r t -> p (r t)"))
 
         def turn(e, u, rb):
             for t in range(4):
@@ -262,201 +266,184 @@ def tile_speaker_pooled_mean_deviation_k5_kernel(
         nc.vector.memset(plane_raw["mean"][:].bitcast(I32), 0)
         nc.scalar.activation(out=warm[:, 1:2], in_=warm[:, 0:1], func=ACT.Sqrt)
 
-        vec_order()
-        vec_turn()
         load_words("dev", 2, 4)
+        vec_order()
+        order_words("dev", 2, 4)
         load_words("dev", 0, 1)
-        vec_unload()
         load_plane(nc.sync, plane_raw["dev"], square_scales, 0, 4)
+        order_words("dev", 0, 1)
         load_plane(nc.sync, attn_plane, attn_scales, 0, 4)
         load_attn(0, 1)
         load_words("dev", 1, 2)
         load_attn(1, 2)
-        load_w("mean", 0, 0, 2)
-        order_words("dev", 0, 1)
+        load_w("dev", 1, 0, 2)
+        vec_turn()
+        vec_unload()
         order_plane("dev", 0, 1)
-        order_plane("dev", 1, 4)
-        order_words("dev", 2, 4)
         load_attn(2, 4)
-        group_w("scalar", "mean", 0, 0, 0, 2)
+        load_plane(nc.sync, plane_raw["mean"], frame_scales, 0, 4)
         pool_run("dev", "all", [0], groups)
+        order_plane("dev", 1, 4)
         order_words("dev", 1, 2)
-        load_plane(nc.gpsimd, plane_raw["mean"], frame_scales, 0, 4)
+        group_w("vector", "dev", 1, 1, 0, 4)
+        group_w("scalar", "dev", 1, 0, 0, 2)
         pool_run("dev", "all", [1], groups)
-        load_words("mean", 2, 4)
-        pool_run("dev", "all", [2, 3], groups[0:1])
-        order_plane("mean", 0, 4)
-        group_w("vector", "mean", 0, 0, 2, 4)
         load_words("mean", 0, 2)
-        group_w("vector", "mean", 0, 1, 0, 4)
-        load_w("mean", 1, 0, 2)
-        finish_pool("scalar", "dev", 0, 0, "all")
+        pool_run("dev", "all", [2, 3], groups[0:1])
         pool_run("dev", "all", [2, 3], groups[1:2])
-        pool_run("dev", "all", [2, 3], groups[2:3])
-        order_words("mean", 2, 4)
-        pool_run("dev", "all", [2, 3], groups[3:4])
         load_w("dev", 0, 0, 2)
-        quantize_w("mean", 0, 1)
+        finish_pool("scalar", "dev", 0, 0, "all")
+        group_w("vector", "dev", 1, 0, 2, 4)
+        quantize_w("dev", 1, 1)
+        pool_run("dev", "all", [2, 3], groups[2:3])
+        finish_pool("scalar", "dev", 0, 1, "all")
+        pool_run("dev", "all", [2, 3], groups[3:4])
+        finish_pool("scalar", "dev", 0, 2, "all")
+        quantize_w("dev", 1, 0)
+        load_words("mean", 2, 4)
         pool_run("dev", "all", [2, 3], groups[4:5])
-        order_words("mean", 0, 2)
+        finish_pool("scalar", "dev", 0, 3, "all")
+        order_plane("mean", 0, 4)
         pool_run("dev", "all", [2, 3], groups[5:6])
         pool_run("dev", "all", [2, 3], groups[6:7])
-        finish_pool("scalar", "dev", 0, 1, "all")
-        quantize_w("mean", 0, 0)
-        finish_pool("scalar", "dev", 0, 2, "all")
-        finish_pool("scalar", "dev", 0, 3, "all")
+        order_words("mean", 0, 2)
+        pool_run("dev", "all", [2, 3], groups[7:8])
+        group_act("vector", "dev", 0, "all", "all")
         finish_pool("scalar", "dev", 1, 0, "all")
         finish_pool("scalar", "dev", 1, 1, "all")
-        group_act("vector", "dev", 0, "all", "all")
-        pool_run("dev", "all", [2, 3], groups[7:8])
         finish_pool("scalar", "dev", 1, 2, "all")
-        finish_pool("scalar", "dev", 1, 3, "all")
-        group_w("scalar", "mean", 1, 0, 0, 2)
-        group_w("vector", "mean", 1, 0, 2, 4)
-        pool_run("mean", "a", [0], groups)
-        pool_run("mean", "a", [1], groups)
-        pool_run("mean", "a", [2, 3], groups[0:1])
-        quantize_act("dev", 0, "all")
-        pool_run("mean", "a", [2, 3], groups[1:2])
-        group_w("vector", "mean", 1, 1, 0, 2)
-        group_act("vector", "dev", 1, "all", "all")
-        pool_run("mean", "a", [2, 3], groups[2:3])
-        pool_run("mean", "a", [2, 3], groups[3:4])
-        pool_run("mean", "a", [2, 3], groups[4:5])
-        group_w("scalar", "dev", 0, 1, 0, 2)
-        finish_pool("scalar", "mean", 0, 0, "a")
-        finish_pool("scalar", "mean", 0, 1, "a")
-        pool_run("mean", "a", [2, 3], groups[5:6])
-        pool_run("mean", "a", [2, 3], groups[6:7])
-        finish_pool("scalar", "mean", 0, 2, "a")
-        finish_pool("scalar", "mean", 0, 3, "a")
-        finish_pool("scalar", "mean", 1, 0, "a")
-        finish_pool("scalar", "mean", 1, 1, "a")
-        pool_run("mean", "a", [2, 3], groups[7:8])
-        pool_run("mean", "b", [0, 1, 2, 3], groups[0:1])
-        finish_pool("scalar", "mean", 1, 2, "a")
-        finish_pool("scalar", "mean", 1, 3, "a")
         group_w("vector", "dev", 0, 0, 0, 2)
-        quantize_act("dev", 1, "all")
-        group_w("vector", "dev", 0, 0, 2, 4)
-        pool_run("mean", "b", [0, 1, 2, 3], groups[1:2])
-        load_w("dev", 1, 0, 2)
-        group_w("scalar", "dev", 1, 0, 0, 2)
-        finish_pool("scalar", "mean", 0, 0, "b")
-        finish_pool("scalar", "mean", 0, 1, "b")
-        pool_run("mean", "b", [0, 1, 2, 3], groups[2:3])
-        pool_run("mean", "b", [0, 1, 2, 3], groups[3:4])
-        finish_pool("scalar", "mean", 0, 2, "b")
-        pool_run("mean", "b", [0, 1, 2, 3], groups[4:5])
-        group_act("vector", "mean", 0, "a")
-        pool_run("mean", "b", [0, 1, 2, 3], groups[5:6])
-        group_w("vector", "dev", 1, 0, 2, 4)
+        finish_pool("scalar", "dev", 1, 3, "all")
+        group_w("scalar", "dev", 0, 0, 2, 4)
+        pool_run("mean", "all", [0], groups)
+        pool_run("mean", "all", [1], groups)
+        quantize_act("dev", 0, "all")
+        group_w("vector", "dev", 0, 1, 0, 2)
+        order_words("mean", 2, 4)
+        group_w("scalar", "dev", 0, 1, 2, 4)
+        pool_run("mean", "all", [2, 3], groups[0:1])
+        load_w("mean", 1, 0, 2)
+        group_act("vector", "dev", 1, "all", "a")
+        load_w("mean", 0, 0, 2)
         quantize_w("dev", 0, 0)
-        group_act("vector", "mean", 1, "a")
-        finish_pool("scalar", "mean", 0, 3, "b")
-        quantize_act("mean", 0, "a")
-        finish_pool("scalar", "mean", 1, 0, "b")
-        quantize_w("dev", 1, 0)
-        finish_pool("scalar", "mean", 1, 1, "b")
-        quantize_act("mean", 1, "a")
-        pool_run("mean", "b", [0, 1, 2, 3], groups[6:7])
-        pool_run("mean", "b", [0, 1, 2, 3], groups[7:8])
+        group_w("vector", "mean", 1, 1, 0, 2)
+        group_act("scalar", "dev", 1, "all", "b")
+        pool_run("mean", "all", [2, 3], groups[1:2])
+        pool_run("mean", "all", [2, 3], groups[2:3])
+        group_w("vector", "mean", 1, 0, 0, 2)
+        pool_run("mean", "all", [2, 3], groups[3:4])
+        group_w("scalar", "mean", 1, 0, 2, 4)
+        quantize_act("dev", 1, "all")
+        pool_run("mean", "all", [2, 3], groups[4:5])
+        pool_run("mean", "all", [2, 3], groups[5:6])
+        finish_pool("vector", "mean", 0, 0, "all")
+        finish_pool("scalar", "mean", 0, 1, "all")
+        group_w("vector", "mean", 0, 0, 0, 4)
+        finish_pool("scalar", "mean", 0, 2, "all")
+        pool_run("mean", "all", [2, 3], groups[6:7])
+        pool_run("mean", "all", [2, 3], groups[7:8])
+        finish_pool("scalar", "mean", 0, 3, "all")
+        finish_pool("scalar", "mean", 1, 0, "all")
         quantize_w("mean", 1, 0)
-        finish_pool("scalar", "mean", 1, 2, "b")
-        embed(0, "a", 0)
-        group_act("vector", "mean", 0, "b")
-        embed(0, "a", 1)
-        embed(0, "a", 2)
-        finish_pool("scalar", "mean", 1, 3, "b")
-        squash(0, "a", 0)
-        group_w("vector", "dev", 0, 1, 2, 4)
-        squash(0, "a", 1)
-        group_act("vector", "mean", 1, "b")
-        squash(0, "a", 2)
+        finish_pool("scalar", "mean", 1, 1, "all")
+        group_act("vector", "mean", 0, "all", "a")
+        embed(0, "all", 0, 0, 1)
+        embed(0, "all", 1, 0, 1)
+        embed(0, "all", 2, 0, 1)
+        group_act("vector", "mean", 0, "all", "b")
+        embed(0, "all", 3, 0, 1)
+        quantize_act("mean", 0, "a")
+        finish_pool("scalar", "mean", 1, 2, "all")
         quantize_act("mean", 0, "b")
-        apply_gain("scalar", 0, "a", 0)
+        finish_pool("scalar", "mean", 1, 3, "all")
+        quantize_w("mean", 0, 0)
+        group_act("vector", "mean", 1, "all", "a")
+        embed(0, "all", 0, 1, 2)
+        embed(0, "all", 1, 1, 2)
+        embed(0, "all", 2, 1, 2)
+        embed(0, "all", 3, 1, 2)
+        group_w("scalar", "mean", 0, 1, 0, 4)
+        group_act("vector", "mean", 1, "all", "b")
+        embed(0, "all", 0, 2, 3)
+        embed(0, "all", 1, 2, 3)
+        quantize_act("mean", 1, "a")
+        embed(0, "all", 2, 2, 3)
         quantize_act("mean", 1, "b")
-        embed(0, "a", 3)
-        squash(0, "a", 3)
-        group_w("vector", "dev", 1, 1, 0, 2)
-        apply_gain("vector", 0, "a", 1)
-        apply_gain("scalar", 0, "a", 2)
-        embed(0, "b", 0)
-        group_w("vector", "dev", 1, 1, 2, 4)
-        apply_gain("vector", 0, "a", 3)
+        embed(0, "all", 3, 2, 3)
+        embed(0, "all", 0, 3, 4)
         quantize_w("dev", 0, 1)
-        group_w("scalar", "mean", 1, 1, 2, 4)
-        squash(0, "b", 0)
-        embed(0, "b", 1)
-        squash(0, "b", 1)
-        quantize_w("dev", 1, 1)
-        embed(0, "b", 2)
-        turn(0, "a", 0)
-        squash(0, "b", 2)
+        group_w("vector", "mean", 1, 1, 2, 4)
+        quantize_w("mean", 0, 1)
+        embed(0, "all", 1, 3, 4)
+        squash(0, "all", 0)
+        embed(0, "all", 2, 3, 4)
+        embed(0, "all", 3, 3, 4)
+        squash(0, "all", 1)
         quantize_w("mean", 1, 1)
-        turn(0, "a", 1)
-        group_y(0, "a")
-        embed(0, "b", 3)
-        apply_gain("vector", 0, "b", 0)
-        unload("scalar", 0, 0)
         embed(1, "a", 0)
-        squash(0, "b", 3)
-        store_rows(nc.sync, 0, 0, 1)
-        quantize_y(0, "a")
-        apply_gain("vector", 0, "b", 1)
-        apply_gain("vector", 0, "b", 2)
-        store_codes(nc.sync, 0, "a")
-        squash(1, "a", 0)
+        squash(0, "all", 2)
         embed(1, "a", 1)
-        apply_gain("vector", 0, "b", 3)
+        squash(0, "all", 3)
+        squash(1, "a", 0)
         embed(1, "a", 2)
-        embed(1, "a", 3)
-        apply_gain("vector", 1, "a", 0)
-        unload("scalar", 0, 1)
+        apply_gain("vector", 0, "all", 0)
         squash(1, "a", 1)
-        group_y(0, "b")
-        store_rows(nc.sync, 0, 1, 2)
-        turn(0, "b", 2)
+        apply_gain("vector", 0, "all", 1)
+        embed(1, "a", 3)
+        apply_gain("vector", 0, "all", 2)
         squash(1, "a", 2)
-        apply_gain("vector", 1, "a", 1)
+        apply_gain("vector", 0, "all", 3)
+        turn(0, "all", 0)
+        apply_gain("vector", 1, "a", 0)
+        turn(0, "all", 1)
         squash(1, "a", 3)
-        quantize_y(0, "b")
-        unload("scalar", 0, 2)
-        turn(0, "b", 3)
+        group_y(0, "all", "a")
+        apply_gain("vector", 1, "a", 1)
+        unload("scalar", 0, 0)
+        turn(0, "all", 2)
+        unload("scalar", 0, 1)
+        turn(0, "all", 3)
+        quantize_y(0, "all", "a")
+        store_codes(nc.sync, 0, "a")
+        group_y(0, "all", "b")
+        apply_gain("scalar", 1, "a", 2)
         embed(1, "b", 0)
+        unload("scalar", 0, 2)
+        store_rows(nc.sync, 0, 0, 1)
+        store_rows(nc.sync, 0, 1, 2)
+        squash(1, "b", 0)
         embed(1, "b", 1)
-        apply_gain("vector", 1, "a", 2)
         apply_gain("vector", 1, "a", 3)
-        unload("scalar", 0, 3)
+        quantize_y(0, "all", "b")
         embed(1, "b", 2)
+        unload("vector", 0, 3)
+        squash(1, "b", 1)
         embed(1, "b", 3)
+        squash(1, "b", 2)
         store_codes(nc.sync, 0, "b")
+        store_rows(nc.sync, 0, 3, 4)
+        group_y(1, "a")
+        apply_gain("vector", 1, "b", 0)
+        quantize_y(1, "a")
+        apply_gain("vector", 1, "b", 1)
         turn(1, "a", 0)
         store_rows(nc.sync, 0, 2, 3)
-        group_y(1, "a")
-        squash(1, "b", 0)
-        store_rows(nc.sync, 0, 3, 4)
-        quantize_y(1, "a")
-        turn(1, "a", 1)
-        apply_gain("vector", 1, "b", 0)
-        squash(1, "b", 1)
-        apply_gain("vector", 1, "b", 1)
-        squash(1, "b", 2)
         apply_gain("vector", 1, "b", 2)
-        store_codes(nc.sync, 1, "a")
+        unload("vector", 1, 0)
+        turn(1, "a", 1)
         squash(1, "b", 3)
-        unload("scalar", 1, 0)
-        apply_gain("vector", 1, "b", 3)
-        unload("vector", 1, 1)
-        store_rows(nc.sync, 1, 0, 1)
-        group_y(1, "b")
+        store_codes(nc.scalar, 1, "a")
+        apply_gain("scalar", 1, "b", 3)
         turn(1, "b", 2)
-        store_rows(nc.sync, 1, 1, 2)
+        group_y(1, "b")
         quantize_y(1, "b")
-        turn(1, "b", 3)
+        store_rows(nc.sync, 1, 0, 1)
+        unload("scalar", 1, 1)
+        store_rows(nc.sync, 1, 1, 2)
         unload("scalar", 1, 2)
-        store_rows(nc.scalar, 1, 2, 3)
+        store_rows(nc.sync, 1, 2, 3)
+        turn(1, "b", 3)
         store_plane([nc.sync] * 4)
-        unload("scalar", 1, 3)
+        unload("vector", 1, 3)
         store_codes(nc.sync, 1, "b")
-        store_rows(nc.sync, 1, 3, 4)
+        store_rows(nc.scalar, 1, 3, 4)

@@ -4,7 +4,7 @@ import concourse.mybir as mybir
 from concourse.masks import make_identity
 
 R, T, F, E = 512, 2048, 1024, 1024
-FLOPS = 2 * R * T * F * 2 + 2 * R * F * E * 2
+FLOPS = 2 * (2 * R * T * F) + 2 * (2 * R * F * E)
 
 F32 = mybir.dt.float32
 BF16 = mybir.dt.bfloat16
@@ -17,8 +17,16 @@ ACT = mybir.ActivationFunctionType
 ALU = mybir.AluOpType
 
 P = 128
-UNITS = [(0, "all"), (1, "a"), (1, "b")]
-G = T // 512
+SLOTS = 4
+HALF = P * SLOTS
+FRAME_PASSES = T // HALF
+BANK = 512
+
+ALL, FIRST, SECOND = slice(0, R), slice(0, R // 2), slice(R // 2, R)
+BOTH, LOW, HIGH = slice(0, 4), slice(0, 2), slice(2, 4)
+MEAN_ROW, DEV_ROW, BIAS_ROW, GAIN_ROW, VEC_ROWS = 0, 2, 32, 34, 36
+TURN_BANK = 4
+VEC_BANK = 7
 
 
 def tile_speaker_pooled_mean_deviation_k5_kernel(
@@ -27,423 +35,361 @@ def tile_speaker_pooled_mean_deviation_k5_kernel(
 ):
     nc = tc.nc
     with ExitStack() as ctx:
-        sb = ctx.enter_context(tc.tile_pool(name="sb", bufs=1))
+        sbuf = ctx.enter_context(tc.tile_pool(name="sbuf", bufs=1))
         psum = ctx.enter_context(tc.psum_pool(name="psum", bufs=1))
         ctx.enter_context(tc.manual_schedule())
 
         def tile(name, shape, dtype):
-            return sb.tile(shape, dtype, name=name, align_bytes=64)
+            return sbuf.tile(shape, dtype, name=name, align_bytes=64)
 
-        bank = [psum.tile([P, 512], F32, name="bank%d" % i) for i in range(8)]
+        copy_on = {"vector": nc.vector.tensor_copy, "scalar": nc.scalar.copy}
+        bank = [psum.tile([P, BANK], F32, name="bank%d" % b) for b in range(8)]
 
-        attn_codes = {}
-        attn_plane = tile("attn_plane", [P, G, 512], U8)
-        words_in = {"dev": square_words, "mean": frame_words}
-        scales_in = {"dev": square_scales, "mean": frame_scales}
-        w_in = {"dev": w_dev, "mean": w_mean}
-        plane_raw = {s: tile("plane_raw_" + s, [P, G, 1024], U8) for s in words_in}
-        plane = {}
-        words_raw = {}
-        words = {}
-        w_raw = {}
-        w_grouped = {}
-        w_codes = {}
-        w_plane = {}
-        act_rows = {}
-        act_grouped = {}
-        act_codes = {}
-        act_plane = {}
+        def quantize(codes, plane, interleaved):
+            nc.vector.quantize_mx(out=codes.bitcast(FP8X4), scales=plane, in_=interleaved)
+
+        def interleave(engine, out, rows):
+            copy_on[engine](
+                out=out.rearrange("p (n i) s -> p n s i", i=4), in_=rows.rearrange("p s (n i) -> p n s i", i=4)
+            )
+
+        vec_rows = tile("vec_rows", [VEC_ROWS, HALF], BF16)
+        vec_ordered = tile("vec_ordered", [P, SLOTS, P], F32)
+        vecs = tile("vecs", [P, SLOTS, VEC_ROWS], F32)
+        ident = tile("ident", [P, P], F32)
+        table_warmup = tile("table_warmup", [P, 8], F32)
+
+        def load_vectors():
+            for row, vec in ((DEV_ROW, var_offset), (MEAN_ROW, rec_mean), (BIAS_ROW, bias), (GAIN_ROW, gain)):
+                nc.sync.dma_start(out=vec_rows[row : row + 2, :], in_=vec.rearrange("(h n) -> h n", h=2))
+
+        def spread_vectors():
+            feature_rows, channel_rows = slice(MEAN_ROW, DEV_ROW + 2), slice(BIAS_ROW, VEC_ROWS)
+            nc.vector.tensor_copy(
+                out=vec_ordered[feature_rows, :, :].rearrange("v j (q c) -> v j q c", c=4),
+                in_=vec_rows[feature_rows, :].rearrange("v (q j c) -> v j q c", j=SLOTS, c=4),
+            )
+            nc.vector.tensor_copy(
+                out=vec_ordered[channel_rows, :, :],
+                in_=vec_rows[channel_rows, :].rearrange("v (m t) -> v t m", t=SLOTS),
+            )
+            for slot in range(SLOTS):
+                nc.tensor.transpose(bank[VEC_BANK][:, P * slot : P * (slot + 1)], vec_ordered[:, slot, :], ident[:])
+
+        def unload_vectors():
+            turned = bank[VEC_BANK][:].rearrange("p (k v) -> p k v", k=SLOTS)
+            nc.vector.tensor_copy(out=vecs[:], in_=turned[:, :, 0:VEC_ROWS])
+
+        def vec_column(row, slot):
+            return vecs[:, slot, row : row + 1]
+
+        words_hbm = {"dev": square_words, "mean": frame_words}
+        attn_codes, pool_raw, pool_codes, pool_plane = {}, {}, {}, {}
+        attn_plane = tile("attn_plane", [P, FRAME_PASSES, R], U8)
+        pool_plane_raw = {stat: tile("pool_plane_raw_" + stat, [P, FRAME_PASSES, F], U8) for stat in words_hbm}
+
+        def load_plane(plane, scales):
+            rows = scales.rearrange("g (q r) n -> r q g n", r=4)
+            for r in range(4):
+                nc.sync.dma_start(out=plane[r:P:32, :, :].bitcast(I32), in_=rows[r].bitcast(I32))
 
         def load_attn(g0, g1):
-            dst = tile("attn_codes_%d" % g0, [P, g1 - g0, 1024], U8)
+            dst = tile("attn_codes_%d" % g0, [P, g1 - g0, 2 * R], U8)
             for g in range(g0, g1):
                 attn_codes[g] = dst[:, g - g0, :]
             nc.sync.dma_start(out=dst[:].bitcast(I32), in_=attn_words[g0:g1].rearrange("g p n -> p g n").bitcast(I32))
 
-        def load_plane(queue, dst, src, g0, g1):
-            rows = src[g0:g1].rearrange("g (q r) n -> r q g n", r=4)
-            for r in range(4):
-                queue.dma_start(out=dst[r:P:32, g0:g1, :].bitcast(I32), in_=rows[r].bitcast(I32))
+        def load_words(stat, g0, g1):
+            raw = tile("pool_raw_%s_%d" % (stat, g0), [P, g1 - g0, 2 * F], U8)
+            pool_raw[stat, g0] = raw
+            src = words_hbm[stat][g0:g1].rearrange("g p n -> p g n")
+            nc.sync.dma_start(out=raw[:].bitcast(I32), in_=src.bitcast(I32))
 
-        def load_words(s, g0, g1):
-            raw = tile("words_raw_%s_%d" % (s, g0), [P, g1 - g0, 2048], U8)
-            words_raw[s, g0] = raw
-            nc.sync.dma_start(out=raw[:].bitcast(I32), in_=words_in[s][g0:g1].rearrange("g p n -> p g n").bitcast(I32))
-
-        def order_words(s, g0, g1):
-            dst = tile("words_%s_%d" % (s, g0), [P, 4, g1 - g0, 512], U8)
+        def order_words(stat, g0, g1):
+            dst = tile("pool_codes_%s_%d" % (stat, g0), [P, SLOTS, g1 - g0, 4 * P], U8)
             for g in range(g0, g1):
                 for h in range(2):
-                    for j in range(4):
-                        words[s, h, j, g] = dst[:, j, g - g0, 256 * h : 256 * (h + 1)]
+                    for j in range(SLOTS):
+                        pool_codes[stat, h, j, g] = dst[:, j, g - g0, 2 * P * h : 2 * P * (h + 1)]
             nc.vector.tensor_copy(
                 out=dst[:].bitcast(I32).rearrange("p j g (q w) -> p j (g q) w", w=2),
-                in_=words_raw[s, g0][:].bitcast(I32).rearrange("p g (q j w) -> p j (g q) w", j=4, w=2),
+                in_=pool_raw[stat, g0][:].bitcast(I32).rearrange("p g (q j w) -> p j (g q) w", j=SLOTS, w=2),
             )
 
-        def order_plane(s, g0, g1):
-            dst = tile("plane_%s_%d" % (s, g0), [P, 4, g1 - g0, 256], U8)
+        def order_plane(stat, g0, g1):
+            dst = tile("pool_plane_%s_%d" % (stat, g0), [P, SLOTS, g1 - g0, 2 * P], U8)
             for g in range(g0, g1):
                 for h in range(2):
-                    for j in range(4):
-                        plane[s, h, j, g] = dst[:, j, g - g0, 128 * h : 128 * (h + 1)]
+                    for j in range(SLOTS):
+                        pool_plane[stat, h, j, g] = dst[:, j, g - g0, P * h : P * (h + 1)]
             nc.vector.tensor_copy(
                 out=dst[:].bitcast(I32).rearrange("p j g q -> p (g q) j"),
-                in_=plane_raw[s][:, g0:g1, :].bitcast(I32).rearrange("p g (q j) -> p (g q) j", j=4),
+                in_=pool_plane_raw[stat][:, g0:g1, :].bitcast(I32).rearrange("p g (q j) -> p (g q) j", j=SLOTS),
             )
 
-        def load_w(s, h, e0, e1):
-            raw = tile("w_raw_%s_%d_%d" % (s, h, e0), [P, 4, 512 * (e1 - e0)], BF16)
-            for e in range(e0, e1):
-                w_raw[s, h, e] = raw[:, :, 512 * (e - e0) : 512 * (e - e0 + 1)]
-            rows = w_in[s][512 * h : 512 * (h + 1), 512 * e0 : 512 * e1].rearrange("(q j c) e -> c q j e", j=4, c=4)
-            for c in range(4):
-                nc.sync.dma_start(out=raw[c:P:4, :, :], in_=rows[c])
+        def pool_passes(stat, h, j, g0, g1):
+            for g in range(g0, g1):
+                nc.tensor.matmul_mx(
+                    out=bank[SLOTS * h + j][:],
+                    lhsT=pool_codes[stat, h, j, g].bitcast(FP4X4), lhsT_scale=pool_plane[stat, h, j, g],
+                    rhs=attn_codes[g].bitcast(FP4X4), rhs_scale=attn_plane[:, g, :],
+                    start=(g == 0), stop=(g == FRAME_PASSES - 1),
+                )
 
-        def group_w(engine, s, h, e, t0=0, t1=4):
-            if (s, h, e) not in w_grouped:
-                w_grouped[s, h, e] = tile("w_grouped_%s_%d_%d" % (s, h, e), [P, 4, P, 4], BF16)
-            src = w_raw[s, h, e].rearrange("p j (m a t) -> p m t a j", a=2, t=4)[:, :, t0:t1]
-            out = w_grouped[s, h, e][:].rearrange("p t (m a) j -> p m t a j", a=2)[:, :, t0:t1]
-            if engine == "vector":
-                nc.vector.tensor_copy(out=out, in_=src)
-            else:
-                nc.scalar.copy(out=out, in_=src)
+        feature_groups = [(h, j) for h in range(2) for j in range(SLOTS)]
+        stat_halves = [(stat, h) for stat in words_hbm for h in range(2)]
+        stat_rows = {k: tile("stat_rows_%s_%d" % k, [P, SLOTS, R], BF16) for k in stat_halves}
+        stat_mixed = {k: tile("stat_mixed_%s_%d" % k, [P, R, SLOTS], BF16) for k in stat_halves}
+        stat_codes = {k: tile("stat_codes_%s_%d" % k, [P, R], U32) for k in stat_halves}
+        stat_plane = {k: tile("stat_plane_%s_%d" % k, [P, R], U8) for k in stat_halves}
 
-        def quantize(codes, scales, grouped):
-            nc.vector.quantize_mx(out=codes.bitcast(FP8X4), scales=scales, in_=grouped)
-
-        def quantize_w(s, h, e):
-            w_codes[s, h, e] = tile("w_codes_%s_%d_%d" % (s, h, e), [P, 512], U32)
-            w_plane[s, h, e] = tile("w_plane_%s_%d_%d" % (s, h, e), [P, 512], U8)
-            quantize(w_codes[s, h, e][:], w_plane[s, h, e][:], w_grouped[s, h, e][:].rearrange("p t m j -> p (t m j)"))
-
-        spans = {"all": slice(0, R), "a": slice(0, 256), "b": slice(256, 512), "c": slice(256, 384), "d": slice(384, 512)}
-
-        def pool_pass(s, h, j, g, u):
-            rows = spans[u]
-            nc.tensor.matmul_mx(
-                out=bank[4 * h + j][:, rows],
-                lhsT=words[s, h, j, g].bitcast(FP4X4), lhsT_scale=plane[s, h, j, g],
-                rhs=attn_codes[g][:, 2 * rows.start : 2 * rows.stop].bitcast(FP4X4), rhs_scale=attn_plane[:, g, rows],
-                start=(g == 0), stop=(g == G - 1),
+        def finish_dev(h, j):
+            nc.scalar.activation(
+                out=stat_rows["dev", h][:, j, :], in_=bank[SLOTS * h + j][:],
+                func=ACT.Sqrt, bias=vec_column(DEV_ROW + h, j),
             )
 
-        for s, us in (("dev", ["all"]), ("mean", ["all"])):
-            for h in range(2):
-                act_codes[s, h] = tile("act_codes_%s_%d" % (s, h), [P, R], U32)
-                act_plane[s, h] = tile("act_plane_%s_%d" % (s, h), [P, R], U8)
-                for u in us:
-                    n = spans[u].stop - spans[u].start
-                    act_rows[s, h, u] = tile("act_rows_%s_%d_%s" % (s, h, u), [P, 4, n], BF16)
-                    act_grouped[s, h, u] = tile("act_grouped_%s_%d_%s" % (s, h, u), [P, n, 4], BF16)
-
-        def finish_pool(engine, s, h, j, u):
-            col = (2 if s == "dev" else 0) + h
-            out, acc, offset = act_rows[s, h, u][:, j, :], bank[4 * h + j][:, spans[u]], vecs[:, j, col : col + 1]
+        def finish_mean(engine, h, j):
+            out, acc, offset = stat_rows["mean", h][:, j, :], bank[SLOTS * h + j][:], vec_column(MEAN_ROW + h, j)
             if engine == "vector":
                 nc.vector.tensor_scalar(out=out, in0=acc, scalar1=offset, scalar2=None, op0=ALU.add)
             else:
-                nc.scalar.activation(out=out, in_=acc, func=ACT.Sqrt if s == "dev" else ACT.Identity, bias=offset)
+                nc.scalar.activation(out=out, in_=acc, func=ACT.Identity, bias=offset)
 
-        def interleave(engine, out, rows):
-            out = out.rearrange("p (r i) j -> p r j i", i=4)
-            rows = rows.rearrange("p j (r i) -> p r j i", i=4)
-            if engine == "vector":
-                nc.vector.tensor_copy(out=out, in_=rows)
-            else:
-                nc.scalar.copy(out=out, in_=rows)
+        def interleave_stat(stat, h, segs):
+            interleave("vector", stat_mixed[stat, h][:, segs, :], stat_rows[stat, h][:, :, segs])
 
-        def group_act(engine, s, h, u, part=None):
-            rows = spans[part] if part else slice(0, 256)
-            interleave(engine, act_grouped[s, h, u][:, rows, :], act_rows[s, h, u][:, :, rows])
+        def quantize_stat(stat, h, segs):
+            mixed = stat_mixed[stat, h][:, segs, :].rearrange("p r j -> p (r j)")
+            quantize(stat_codes[stat, h][:, segs], stat_plane[stat, h][:, segs], mixed)
 
-        def quantize_act(s, h, u):
-            quantize(act_codes[s, h][:, spans[u]], act_plane[s, h][:, spans[u]], act_grouped[s, h, "all"][:, spans[u], :].rearrange("p r j -> p (r j)"))
+        w_hbm = {"dev": w_dev, "mean": w_mean}
+        w_tiles = [(stat, h, e) for stat, h in stat_halves for e in range(2)]
+        w_raw = {k: tile("w_raw_%s_%d" % k, [P, SLOTS, E], BF16) for k in stat_halves}
+        w_mixed = {k: tile("w_mixed_%s_%d_%d" % k, [P, SLOTS, P, SLOTS], BF16) for k in w_tiles}
+        w_codes = {k: tile("w_codes_%s_%d_%d" % k, [P, HALF], U32) for k in w_tiles}
+        w_plane = {k: tile("w_plane_%s_%d_%d" % k, [P, HALF], U8) for k in w_tiles}
 
-        passes = [("dev", 0), ("dev", 1), ("mean", 0), ("mean", 1)]
+        def load_w(stat, h):
+            rows = w_hbm[stat][HALF * h : HALF * (h + 1), :].rearrange("(q j c) e -> c q j e", j=SLOTS, c=4)
+            for c in range(4):
+                nc.sync.dma_start(out=w_raw[stat, h][c:P:4, :, :], in_=rows[c])
 
-        def embed(e, u, t, i0=0, i1=4):
-            rows = spans[u]
+        def interleave_w(engine, stat, h, e, slots):
+            src = w_raw[stat, h][:, :, HALF * e : HALF * (e + 1)].rearrange("p j (m a t) -> p m t a j", a=2, t=SLOTS)
+            dst = w_mixed[stat, h, e][:].rearrange("p t (m a) j -> p m t a j", a=2)
+            copy_on[engine](out=dst[:, :, slots], in_=src[:, :, slots])
+
+        def quantize_w(stat, h, e):
+            mixed = w_mixed[stat, h, e][:].rearrange("p t m j -> p (t m j)")
+            quantize(w_codes[stat, h, e][:], w_plane[stat, h, e][:], mixed)
+
+        def embed_pass(e, segs, t, i):
+            stat, h = stat_halves[i]
             cols = slice(P * t, P * (t + 1))
-            for i in range(i0, i1):
-                s, h = passes[i]
-                nc.tensor.matmul_mx(
-                    out=bank[t][:, rows],
-                    lhsT=w_codes[s, h, e][:, cols].bitcast(FP8X4), lhsT_scale=w_plane[s, h, e][:, cols],
-                    rhs=act_codes[s, h][:, rows].bitcast(FP8X4), rhs_scale=act_plane[s, h][:, rows],
-                    start=(i == 0), stop=(i == 3),
-                )
+            nc.tensor.matmul_mx(
+                out=bank[t][:, segs],
+                lhsT=w_codes[stat, h, e][:, cols].bitcast(FP8X4), lhsT_scale=w_plane[stat, h, e][:, cols],
+                rhs=stat_codes[stat, h][:, segs].bitcast(FP8X4), rhs_scale=stat_plane[stat, h][:, segs],
+                start=(i == 0), stop=(i == len(stat_halves) - 1),
+            )
 
-        units = UNITS
-        y_t = {k: tile("y_t%d%s" % k, [P, 4, spans[k[1]].stop - spans[k[1]].start], F32) for k in units}
-        y_grouped = {k: tile("y_grouped%d%s" % k, [P, spans[k[1]].stop - spans[k[1]].start, 4], BF16) for k in units}
+        def embed(e, segs, t):
+            for i in range(len(stat_halves)):
+                embed_pass(e, segs, t, i)
+
+        y_cols_low = tile("y_cols_low", [P, SLOTS, R], F32)
+        y_cols_high = [tile("y_cols_high%d" % u, [P, SLOTS, R // 2], F32) for u in range(2)]
+        y_mixed = [tile("y_mixed%d" % e, [P, R, SLOTS], BF16) for e in range(2)]
         y_codes = [tile("y_codes%d" % e, [P, R], U32) for e in range(2)]
         y_plane = tile("y_plane", [P, 2, R], U8)
-        y_rows = [tile("y_rows%d" % e, [P, 4, 512], F32) for e in range(2)]
+        y_rows = [tile("y_rows%d" % e, [P, R // P, HALF], F32) for e in range(2)]
 
-        def squash(e, u, t):
-            nc.scalar.activation(out=y_t[e, u][:, t, :], in_=bank[t][:, spans[u]], func=ACT.Tanh, bias=vecs[:, t, 32 + e : 33 + e])
+        def y_cols(e, segs):
+            if e == 0:
+                return y_cols_low[:, :, segs]
+            first = segs.start % (R // 2)
+            return y_cols_high[segs.start // (R // 2)][:, :, first : first + segs.stop - segs.start]
 
-        def apply_gain(engine, e, u, t):
-            if engine == "vector":
-                nc.vector.tensor_scalar(
-                    out=y_t[e, u][:, t, :], in0=y_t[e, u][:, t, :],
-                    scalar1=vecs[:, t, 34 + e : 35 + e], scalar2=None, op0=ALU.mult,
-                )
-            else:
-                nc.scalar.activation(out=y_t[e, u][:, t, :], in_=y_t[e, u][:, t, :], func=ACT.Copy, scale=vecs[:, t, 34 + e : 35 + e])
-
-        def group_y(e, u, part=None):
-            rows = spans[part] if part else slice(0, 256)
-            interleave("vector", y_grouped[e, u][:, rows, :], y_t[e, u][:, :, rows])
-
-        def quantize_y(e, u, part=None):
-            rows = spans[part] if part else slice(0, 256)
-            at = spans[part or u]
-            quantize(y_codes[e][:, at], y_plane[:, e, at], y_grouped[e, u][:, rows, :].rearrange("p r t -> p (r t)"))
-
-        def turn(e, u, rb):
-            for t in range(4):
-                src = y_t[e, u][:, t, P * rb - spans[u].start : P * (rb + 1) - spans[u].start]
-                nc.tensor.transpose(bank[4 + rb][:, P * t : P * (t + 1)], src, ident[:])
-
-        def unload(engine, e, rb):
-            dst = y_rows[e][:, rb, :].rearrange("p (m t) -> p m t", t=4)
-            src = bank[4 + rb][:].rearrange("p (t m) -> p m t", t=4)
-            if engine == "vector":
-                nc.vector.tensor_copy(out=dst, in_=src)
-            else:
-                nc.scalar.copy(out=dst, in_=src)
-
-        def store_rows(queue, e, rb0, rb1):
-            dst = out_0[P * rb0 : P * rb1, 512 * e : 512 * (e + 1)].rearrange("(b p) n -> p b n", p=P)
-            queue.dma_start(out=dst, in_=y_rows[e][:, rb0:rb1, :])
-
-        def store_codes(queue, e, u):
-            dst = out_1[e].rearrange("p m t -> p (m t)").bitcast(I32)
-            queue.dma_start(out=dst[:, spans[u]], in_=y_codes[e][:, spans[u]].bitcast(I32))
-
-        def vec_turn():
-            for j in range(4):
-                nc.tensor.transpose(bank[7][:, P * j : P * (j + 1)], vec_f[:, j, :], ident[:])
-
-        def vec_unload():
-            nc.vector.tensor_copy(out=vecs[:], in_=bank[7][:].rearrange("p (j v) -> p j v", j=4)[:, :, 0:36])
-
-        def pool_run(s, u, gs, groups):
-            for h, j in groups:
-                for g in gs:
-                    pool_pass(s, h, j, g, u)
-
-        groups = [(h, j) for h in range(2) for j in range(4)]
-
-        def store_plane(queues):
-            plane_rows = out_2.rearrange("g (q r) m -> r q g m", r=4)
-            for r in range(4):
-                queues[r].dma_start(out=plane_rows[r].bitcast(I32), in_=y_plane[r:P:32, :, :].bitcast(I32))
-
-        def vec_order():
-            nc.vector.tensor_copy(
-                out=vec_f[0:4, :, :].rearrange("v j (q c) -> v j q c", c=4),
-                in_=vec_rows[0:4, :].rearrange("v (q j c) -> v j q c", j=4, c=4),
+        def squash(e, segs, t):
+            nc.scalar.activation(
+                out=y_cols(e, segs)[:, t, :], in_=bank[t][:, segs], func=ACT.Tanh, bias=vec_column(BIAS_ROW + e, t)
             )
-            nc.vector.tensor_copy(out=vec_f[32:36, :, :], in_=vec_rows[32:36, :].rearrange("v (m t) -> v t m", t=4))
 
-        vec_rows = tile("vec_rows", [36, 512], BF16)
-        vec_f = tile("vec_f", [P, 4, P], F32)
-        vecs = tile("vecs", [P, 4, 36], F32)
-        ident = tile("ident", [P, P], F32)
-        warm = tile("warm", [P, 8], F32)
+        def apply_gain(engine, e, segs, t):
+            y, factor = y_cols(e, segs)[:, t, :], vec_column(GAIN_ROW + e, t)
+            if engine == "vector":
+                nc.vector.tensor_scalar(out=y, in0=y, scalar1=factor, scalar2=None, op0=ALU.mult)
+            else:
+                nc.scalar.activation(out=y, in_=y, func=ACT.Copy, scale=factor)
+
+        def interleave_y(e, segs):
+            interleave("vector", y_mixed[e][:, segs, :], y_cols(e, segs))
+
+        def quantize_y(e, segs):
+            quantize(y_codes[e][:, segs], y_plane[:, e, segs], y_mixed[e][:, segs, :].rearrange("p r t -> p (r t)"))
+
+        def turn(e, block):
+            src = y_cols(e, slice(P * block, P * (block + 1)))
+            for t in range(SLOTS):
+                nc.tensor.transpose(bank[TURN_BANK + block][:, P * t : P * (t + 1)], src[:, t, :], ident[:])
+
+        def unload(engine, e, block):
+            copy_on[engine](
+                out=y_rows[e][:, block, :].rearrange("r (p t) -> r p t", t=SLOTS),
+                in_=bank[TURN_BANK + block][:].rearrange("r (t p) -> r p t", t=SLOTS),
+            )
+
+        def store_rows(e, block):
+            dst = out_0[P * block : P * (block + 1), HALF * e : HALF * (e + 1)]
+            nc.sync.dma_start(out=dst, in_=y_rows[e][:, block, :])
+
+        def store_codes(queue, e, segs):
+            dst = out_1[e].rearrange("p m t -> p (m t)").bitcast(I32)
+            queue.dma_start(out=dst[:, segs], in_=y_codes[e][:, segs].bitcast(I32))
+
+        def store_plane():
+            rows = out_2.rearrange("g (q r) m -> r q g m", r=4)
+            for r in range(4):
+                nc.sync.dma_start(out=rows[r].bitcast(I32), in_=y_plane[r:P:32, :, :].bitcast(I32))
 
         make_identity(nc, ident[:])
-        for row, vec in ((2, var_offset), (0, rec_mean), (32, bias), (34, gain)):
-            nc.scalar.dma_start(out=vec_rows[row : row + 2, :], in_=vec.rearrange("(h n) -> h n", h=2))
-        nc.vector.memset(plane_raw["dev"][:].bitcast(I32), 0)
+        nc.vector.memset(pool_plane_raw["dev"][:].bitcast(I32), 0)
         nc.vector.memset(attn_plane[:].bitcast(I32), 0)
-        nc.vector.memset(warm[:, 0:1], 1.0)
-        nc.vector.memset(vec_f[:], 0.0)
-        nc.vector.memset(plane_raw["mean"][:].bitcast(I32), 0)
-        nc.scalar.activation(out=warm[:, 1:2], in_=warm[:, 0:1], func=ACT.Sqrt)
+        nc.vector.memset(table_warmup[:, 0:1], 1.0)
+        nc.vector.memset(vec_ordered[:], 0.0)
+        nc.vector.memset(pool_plane_raw["mean"][:].bitcast(I32), 0)
+        nc.scalar.activation(out=table_warmup[:, 1:2], in_=table_warmup[:, 0:1], func=ACT.Sqrt)
 
-        load_words("dev", 2, 4)
-        vec_order()
-        order_words("dev", 2, 4)
-        load_words("dev", 0, 1)
-        load_plane(nc.sync, plane_raw["dev"], square_scales, 0, 4)
-        order_words("dev", 0, 1)
-        load_plane(nc.sync, attn_plane, attn_scales, 0, 4)
         load_attn(0, 1)
+        load_words("dev", 0, 1)
+        load_vectors()
+        load_words("dev", 2, 4)
+        load_plane(pool_plane_raw["dev"], square_scales)
+        load_plane(attn_plane, attn_scales)
+        load_w("dev", 0)
         load_words("dev", 1, 2)
         load_attn(1, 2)
-        load_w("dev", 1, 0, 2)
-        vec_turn()
-        vec_unload()
-        order_plane("dev", 0, 1)
+        load_w("dev", 1)
         load_attn(2, 4)
-        load_plane(nc.sync, plane_raw["mean"], frame_scales, 0, 4)
-        pool_run("dev", "all", [0], groups)
-        order_plane("dev", 1, 4)
-        order_words("dev", 1, 2)
-        group_w("vector", "dev", 1, 1, 0, 4)
-        group_w("scalar", "dev", 1, 0, 0, 2)
-        pool_run("dev", "all", [1], groups)
         load_words("mean", 0, 2)
-        pool_run("dev", "all", [2, 3], groups[0:1])
-        pool_run("dev", "all", [2, 3], groups[1:2])
-        load_w("dev", 0, 0, 2)
-        finish_pool("scalar", "dev", 0, 0, "all")
-        group_w("vector", "dev", 1, 0, 2, 4)
-        quantize_w("dev", 1, 1)
-        pool_run("dev", "all", [2, 3], groups[2:3])
-        finish_pool("scalar", "dev", 0, 1, "all")
-        pool_run("dev", "all", [2, 3], groups[3:4])
-        finish_pool("scalar", "dev", 0, 2, "all")
-        quantize_w("dev", 1, 0)
+        load_plane(pool_plane_raw["mean"], frame_scales)
+        load_w("mean", 0)
         load_words("mean", 2, 4)
-        pool_run("dev", "all", [2, 3], groups[4:5])
-        finish_pool("scalar", "dev", 0, 3, "all")
-        order_plane("mean", 0, 4)
-        pool_run("dev", "all", [2, 3], groups[5:6])
-        pool_run("dev", "all", [2, 3], groups[6:7])
-        order_words("mean", 0, 2)
-        pool_run("dev", "all", [2, 3], groups[7:8])
-        group_act("vector", "dev", 0, "all", "all")
-        finish_pool("scalar", "dev", 1, 0, "all")
-        finish_pool("scalar", "dev", 1, 1, "all")
-        finish_pool("scalar", "dev", 1, 2, "all")
-        group_w("vector", "dev", 0, 0, 0, 2)
-        finish_pool("scalar", "dev", 1, 3, "all")
-        group_w("scalar", "dev", 0, 0, 2, 4)
-        pool_run("mean", "all", [0], groups)
-        pool_run("mean", "all", [1], groups)
-        quantize_act("dev", 0, "all")
-        group_w("vector", "dev", 0, 1, 0, 2)
-        order_words("mean", 2, 4)
-        group_w("scalar", "dev", 0, 1, 2, 4)
-        pool_run("mean", "all", [2, 3], groups[0:1])
-        load_w("mean", 1, 0, 2)
-        group_act("vector", "dev", 1, "all", "a")
-        load_w("mean", 0, 0, 2)
-        quantize_w("dev", 0, 0)
-        group_w("vector", "mean", 1, 1, 0, 2)
-        group_act("scalar", "dev", 1, "all", "b")
-        pool_run("mean", "all", [2, 3], groups[1:2])
-        pool_run("mean", "all", [2, 3], groups[2:3])
-        group_w("vector", "mean", 1, 0, 0, 2)
-        pool_run("mean", "all", [2, 3], groups[3:4])
-        group_w("scalar", "mean", 1, 0, 2, 4)
-        quantize_act("dev", 1, "all")
-        pool_run("mean", "all", [2, 3], groups[4:5])
-        pool_run("mean", "all", [2, 3], groups[5:6])
-        finish_pool("vector", "mean", 0, 0, "all")
-        finish_pool("scalar", "mean", 0, 1, "all")
-        group_w("vector", "mean", 0, 0, 0, 4)
-        finish_pool("scalar", "mean", 0, 2, "all")
-        pool_run("mean", "all", [2, 3], groups[6:7])
-        pool_run("mean", "all", [2, 3], groups[7:8])
-        finish_pool("scalar", "mean", 0, 3, "all")
-        finish_pool("scalar", "mean", 1, 0, "all")
-        quantize_w("mean", 1, 0)
-        finish_pool("scalar", "mean", 1, 1, "all")
-        group_act("vector", "mean", 0, "all", "a")
-        embed(0, "all", 0, 0, 1)
-        embed(0, "all", 1, 0, 1)
-        embed(0, "all", 2, 0, 1)
-        group_act("vector", "mean", 0, "all", "b")
-        embed(0, "all", 3, 0, 1)
-        quantize_act("mean", 0, "a")
-        finish_pool("scalar", "mean", 1, 2, "all")
-        quantize_act("mean", 0, "b")
-        finish_pool("scalar", "mean", 1, 3, "all")
-        quantize_w("mean", 0, 0)
-        group_act("vector", "mean", 1, "all", "a")
-        embed(0, "all", 0, 1, 2)
-        embed(0, "all", 1, 1, 2)
-        embed(0, "all", 2, 1, 2)
-        embed(0, "all", 3, 1, 2)
-        group_w("scalar", "mean", 0, 1, 0, 4)
-        group_act("vector", "mean", 1, "all", "b")
-        embed(0, "all", 0, 2, 3)
-        embed(0, "all", 1, 2, 3)
-        quantize_act("mean", 1, "a")
-        embed(0, "all", 2, 2, 3)
-        quantize_act("mean", 1, "b")
-        embed(0, "all", 3, 2, 3)
-        embed(0, "all", 0, 3, 4)
+        load_w("mean", 1)
+
+        spread_vectors()
+        order_words("dev", 0, 1)
+        unload_vectors()
+        order_plane("dev", 0, 1)
+        for h, j in feature_groups:
+            pool_passes("dev", h, j, 0, 1)
+        order_words("dev", 2, 4)
+        order_plane("dev", 1, 4)
+        interleave_w("vector", "dev", 0, 0, LOW)
+        interleave_w("scalar", "dev", 0, 1, LOW)
+        order_words("dev", 1, 2)
+        for h, j in feature_groups:
+            pool_passes("dev", h, j, 1, 2)
+        interleave_w("scalar", "dev", 0, 0, HIGH)
+        interleave_w("vector", "dev", 0, 1, HIGH)
         quantize_w("dev", 0, 1)
-        group_w("vector", "mean", 1, 1, 2, 4)
+        interleave_w("scalar", "dev", 1, 0, LOW)
+
+        for h, j in feature_groups:
+            pool_passes("dev", h, j, 2, 4)
+            finish_dev(h, j)
+        quantize_w("dev", 0, 0)
+        interleave_w("vector", "dev", 1, 1, BOTH)
+        interleave_w("vector", "dev", 1, 0, HIGH)
+        quantize_w("dev", 1, 1)
+        order_words("mean", 0, 2)
+        order_plane("mean", 0, 4)
+        quantize_w("dev", 1, 0)
+
+        for g in range(2):
+            for h, j in feature_groups:
+                pool_passes("mean", h, j, g, g + 1)
+        interleave_stat("dev", 0, ALL)
+        interleave_w("scalar", "mean", 0, 0, LOW)
+        interleave_w("vector", "mean", 0, 0, HIGH)
+        order_words("mean", 2, 4)
+        interleave_w("scalar", "mean", 0, 1, LOW)
+        quantize_stat("dev", 0, ALL)
+        interleave_stat("dev", 1, FIRST)
+        quantize_w("mean", 0, 0)
+        interleave_w("scalar", "mean", 1, 0, LOW)
+        interleave_w("vector", "mean", 1, 0, HIGH)
+        interleave_stat("dev", 1, SECOND)
+        interleave_w("vector", "mean", 1, 1, LOW)
+        quantize_w("mean", 1, 0)
+        quantize_stat("dev", 1, ALL)
+
+        for h, j in feature_groups:
+            pool_passes("mean", h, j, 2, 4)
+            finish_mean("vector" if (h, j) == (1, 0) else "scalar", h, j)
+        for h in range(2):
+            for segs in (FIRST, SECOND):
+                interleave_stat("mean", h, segs)
+            for segs in (FIRST, SECOND):
+                quantize_stat("mean", h, segs)
+        interleave_w("scalar", "mean", 0, 1, HIGH)
+        interleave_w("vector", "mean", 1, 1, HIGH)
         quantize_w("mean", 0, 1)
-        embed(0, "all", 1, 3, 4)
-        squash(0, "all", 0)
-        embed(0, "all", 2, 3, 4)
-        embed(0, "all", 3, 3, 4)
-        squash(0, "all", 1)
         quantize_w("mean", 1, 1)
-        embed(1, "a", 0)
-        squash(0, "all", 2)
-        embed(1, "a", 1)
-        squash(0, "all", 3)
-        squash(1, "a", 0)
-        embed(1, "a", 2)
-        apply_gain("vector", 0, "all", 0)
-        squash(1, "a", 1)
-        apply_gain("vector", 0, "all", 1)
-        embed(1, "a", 3)
-        apply_gain("vector", 0, "all", 2)
-        squash(1, "a", 2)
-        apply_gain("vector", 0, "all", 3)
-        turn(0, "all", 0)
-        apply_gain("vector", 1, "a", 0)
-        turn(0, "all", 1)
-        squash(1, "a", 3)
-        group_y(0, "all", "a")
-        apply_gain("vector", 1, "a", 1)
-        unload("scalar", 0, 0)
-        turn(0, "all", 2)
-        unload("scalar", 0, 1)
-        turn(0, "all", 3)
-        quantize_y(0, "all", "a")
-        store_codes(nc.sync, 0, "a")
-        group_y(0, "all", "b")
-        apply_gain("scalar", 1, "a", 2)
-        embed(1, "b", 0)
-        unload("scalar", 0, 2)
-        store_rows(nc.sync, 0, 0, 1)
-        store_rows(nc.sync, 0, 1, 2)
-        squash(1, "b", 0)
-        embed(1, "b", 1)
-        apply_gain("vector", 1, "a", 3)
-        quantize_y(0, "all", "b")
-        embed(1, "b", 2)
-        unload("vector", 0, 3)
-        squash(1, "b", 1)
-        embed(1, "b", 3)
-        squash(1, "b", 2)
-        store_codes(nc.sync, 0, "b")
-        store_rows(nc.sync, 0, 3, 4)
-        group_y(1, "a")
-        apply_gain("vector", 1, "b", 0)
-        quantize_y(1, "a")
-        apply_gain("vector", 1, "b", 1)
-        turn(1, "a", 0)
-        store_rows(nc.sync, 0, 2, 3)
-        apply_gain("vector", 1, "b", 2)
+
+        for i in range(len(stat_halves)):
+            for t in range(SLOTS):
+                embed_pass(0, ALL, t, i)
+        for t in range(SLOTS):
+            squash(0, ALL, t)
+            apply_gain("vector", 0, ALL, t)
+
+        for t in range(SLOTS):
+            embed(1, FIRST, t)
+            squash(1, FIRST, t)
+        for block in range(R // P):
+            turn(0, block)
+        apply_gain("vector", 1, FIRST, 0)
+        interleave_y(0, FIRST)
+        apply_gain("vector", 1, FIRST, 1)
+        quantize_y(0, FIRST)
+        store_codes(nc.sync, 0, FIRST)
+        interleave_y(0, SECOND)
+        apply_gain("vector", 1, FIRST, 2)
+        quantize_y(0, SECOND)
+        for block in range(2):
+            unload("scalar", 0, block)
+            store_rows(0, block)
+        store_codes(nc.sync, 0, SECOND)
+        apply_gain("scalar", 1, FIRST, 3)
+        unload("vector", 0, 2)
+        store_rows(0, 2)
+
+        for t in range(SLOTS):
+            embed(1, SECOND, t)
+        interleave_y(1, FIRST)
+        squash(1, SECOND, 0)
+        unload("scalar", 0, 3)
+        store_rows(0, 3)
+        apply_gain("vector", 1, SECOND, 0)
+        quantize_y(1, FIRST)
+        for t in range(1, SLOTS):
+            squash(1, SECOND, t)
+        for t in range(1, SLOTS - 1):
+            apply_gain("vector", 1, SECOND, t)
+        store_codes(nc.scalar, 1, FIRST)
+        apply_gain("scalar", 1, SECOND, SLOTS - 1)
+        for block in range(R // P):
+            turn(1, block)
         unload("vector", 1, 0)
-        turn(1, "a", 1)
-        squash(1, "b", 3)
-        store_codes(nc.scalar, 1, "a")
-        apply_gain("scalar", 1, "b", 3)
-        turn(1, "b", 2)
-        group_y(1, "b")
-        quantize_y(1, "b")
-        store_rows(nc.sync, 1, 0, 1)
-        unload("scalar", 1, 1)
-        store_rows(nc.sync, 1, 1, 2)
-        unload("scalar", 1, 2)
-        store_rows(nc.sync, 1, 2, 3)
-        turn(1, "b", 3)
-        store_plane([nc.sync] * 4)
-        unload("vector", 1, 3)
-        store_codes(nc.sync, 1, "b")
-        store_rows(nc.scalar, 1, 3, 4)
+        store_rows(1, 0)
+        interleave_y(1, SECOND)
+        quantize_y(1, SECOND)
+        for block in range(1, R // P - 1):
+            unload("scalar", 1, block)
+            store_rows(1, block)
+        store_codes(nc.sync, 1, SECOND)
+        unload("scalar", 1, R // P - 1)
+        store_rows(1, R // P - 1)
+        store_plane()

from contextlib import ExitStack

import concourse.mybir as mybir
from concourse.masks import make_identity

R, T, F, E = 512, 2048, 1024, 1024
FLOPS = 2 * (2 * R * T * F) + 2 * (2 * R * F * E)

F32 = mybir.dt.float32
BF16 = mybir.dt.bfloat16
I32 = mybir.dt.int32
U32 = mybir.dt.uint32
U8 = mybir.dt.uint8
FP4X4 = mybir.dt.float4_e2m1fn_x4
FP8X4 = mybir.dt.float8_e4m3fn_x4
ACT = mybir.ActivationFunctionType
ALU = mybir.AluOpType

P = 128
SLOTS = 4
HALF = P * SLOTS
FRAME_PASSES = T // HALF
BANK = 512

ALL, FIRST, SECOND = slice(0, R), slice(0, R // 2), slice(R // 2, R)
BOTH, LOW, HIGH = slice(0, 4), slice(0, 2), slice(2, 4)
MEAN_ROW, DEV_ROW, BIAS_ROW, GAIN_ROW, VEC_ROWS = 0, 2, 32, 34, 36
TURN_BANK = 4
VEC_BANK = 7


def tile_speaker_pooled_mean_deviation_k5_kernel(
    tc, attn_words, attn_scales, frame_words, frame_scales, square_words, square_scales,
    rec_mean, var_offset, w_mean, w_dev, bias, gain, out_0, out_1, out_2,
):
    nc = tc.nc
    with ExitStack() as ctx:
        sbuf = ctx.enter_context(tc.tile_pool(name="sbuf", bufs=1))
        psum = ctx.enter_context(tc.psum_pool(name="psum", bufs=1))
        ctx.enter_context(tc.manual_schedule())

        def tile(name, shape, dtype):
            return sbuf.tile(shape, dtype, name=name, align_bytes=64)

        copy_on = {"vector": nc.vector.tensor_copy, "scalar": nc.scalar.copy}
        bank = [psum.tile([P, BANK], F32, name="bank%d" % b) for b in range(8)]

        def quantize(codes, plane, interleaved):
            nc.vector.quantize_mx(out=codes.bitcast(FP8X4), scales=plane, in_=interleaved)

        def interleave(engine, out, rows):
            copy_on[engine](
                out=out.rearrange("p (n i) s -> p n s i", i=4), in_=rows.rearrange("p s (n i) -> p n s i", i=4)
            )

        vec_rows = tile("vec_rows", [VEC_ROWS, HALF], BF16)
        vec_ordered = tile("vec_ordered", [P, SLOTS, P], F32)
        vecs = tile("vecs", [P, SLOTS, VEC_ROWS], F32)
        ident = tile("ident", [P, P], F32)
        table_warmup = tile("table_warmup", [P, 8], F32)

        def load_vectors():
            for row, vec in ((DEV_ROW, var_offset), (MEAN_ROW, rec_mean), (BIAS_ROW, bias), (GAIN_ROW, gain)):
                nc.sync.dma_start(out=vec_rows[row : row + 2, :], in_=vec.rearrange("(h n) -> h n", h=2))

        def spread_vectors():
            feature_rows, channel_rows = slice(MEAN_ROW, DEV_ROW + 2), slice(BIAS_ROW, VEC_ROWS)
            nc.vector.tensor_copy(
                out=vec_ordered[feature_rows, :, :].rearrange("v j (q c) -> v j q c", c=4),
                in_=vec_rows[feature_rows, :].rearrange("v (q j c) -> v j q c", j=SLOTS, c=4),
            )
            nc.vector.tensor_copy(
                out=vec_ordered[channel_rows, :, :],
                in_=vec_rows[channel_rows, :].rearrange("v (m t) -> v t m", t=SLOTS),
            )
            for slot in range(SLOTS):
                nc.tensor.transpose(bank[VEC_BANK][:, P * slot : P * (slot + 1)], vec_ordered[:, slot, :], ident[:])

        def unload_vectors():
            turned = bank[VEC_BANK][:].rearrange("p (k v) -> p k v", k=SLOTS)
            nc.vector.tensor_copy(out=vecs[:], in_=turned[:, :, 0:VEC_ROWS])

        def vec_column(row, slot):
            return vecs[:, slot, row : row + 1]

        words_hbm = {"dev": square_words, "mean": frame_words}
        attn_codes, pool_raw, pool_codes, pool_plane = {}, {}, {}, {}
        attn_plane = tile("attn_plane", [P, FRAME_PASSES, R], U8)
        pool_plane_raw = {stat: tile("pool_plane_raw_" + stat, [P, FRAME_PASSES, F], U8) for stat in words_hbm}

        def load_plane(plane, scales):
            rows = scales.rearrange("g (q r) n -> r q g n", r=4)
            for r in range(4):
                nc.sync.dma_start(out=plane[r:P:32, :, :].bitcast(I32), in_=rows[r].bitcast(I32))

        def load_attn(g0, g1):
            dst = tile("attn_codes_%d" % g0, [P, g1 - g0, 2 * R], U8)
            for g in range(g0, g1):
                attn_codes[g] = dst[:, g - g0, :]
            nc.sync.dma_start(out=dst[:].bitcast(I32), in_=attn_words[g0:g1].rearrange("g p n -> p g n").bitcast(I32))

        def load_words(stat, g0, g1):
            raw = tile("pool_raw_%s_%d" % (stat, g0), [P, g1 - g0, 2 * F], U8)
            pool_raw[stat, g0] = raw
            src = words_hbm[stat][g0:g1].rearrange("g p n -> p g n")
            nc.sync.dma_start(out=raw[:].bitcast(I32), in_=src.bitcast(I32))

        def order_words(stat, g0, g1):
            dst = tile("pool_codes_%s_%d" % (stat, g0), [P, SLOTS, g1 - g0, 4 * P], U8)
            for g in range(g0, g1):
                for h in range(2):
                    for j in range(SLOTS):
                        pool_codes[stat, h, j, g] = dst[:, j, g - g0, 2 * P * h : 2 * P * (h + 1)]
            nc.vector.tensor_copy(
                out=dst[:].bitcast(I32).rearrange("p j g (q w) -> p j (g q) w", w=2),
                in_=pool_raw[stat, g0][:].bitcast(I32).rearrange("p g (q j w) -> p j (g q) w", j=SLOTS, w=2),
            )

        def order_plane(stat, g0, g1):
            dst = tile("pool_plane_%s_%d" % (stat, g0), [P, SLOTS, g1 - g0, 2 * P], U8)
            for g in range(g0, g1):
                for h in range(2):
                    for j in range(SLOTS):
                        pool_plane[stat, h, j, g] = dst[:, j, g - g0, P * h : P * (h + 1)]
            nc.vector.tensor_copy(
                out=dst[:].bitcast(I32).rearrange("p j g q -> p (g q) j"),
                in_=pool_plane_raw[stat][:, g0:g1, :].bitcast(I32).rearrange("p g (q j) -> p (g q) j", j=SLOTS),
            )

        def pool_passes(stat, h, j, g0, g1):
            for g in range(g0, g1):
                nc.tensor.matmul_mx(
                    out=bank[SLOTS * h + j][:],
                    lhsT=pool_codes[stat, h, j, g].bitcast(FP4X4), lhsT_scale=pool_plane[stat, h, j, g],
                    rhs=attn_codes[g].bitcast(FP4X4), rhs_scale=attn_plane[:, g, :],
                    start=(g == 0), stop=(g == FRAME_PASSES - 1),
                )

        feature_groups = [(h, j) for h in range(2) for j in range(SLOTS)]
        stat_halves = [(stat, h) for stat in words_hbm for h in range(2)]
        stat_rows = {k: tile("stat_rows_%s_%d" % k, [P, SLOTS, R], BF16) for k in stat_halves}
        stat_mixed = {k: tile("stat_mixed_%s_%d" % k, [P, R, SLOTS], BF16) for k in stat_halves}
        stat_codes = {k: tile("stat_codes_%s_%d" % k, [P, R], U32) for k in stat_halves}
        stat_plane = {k: tile("stat_plane_%s_%d" % k, [P, R], U8) for k in stat_halves}

        def finish_dev(h, j):
            nc.scalar.activation(
                out=stat_rows["dev", h][:, j, :], in_=bank[SLOTS * h + j][:],
                func=ACT.Sqrt, bias=vec_column(DEV_ROW + h, j),
            )

        def finish_mean(engine, h, j):
            out, acc, offset = stat_rows["mean", h][:, j, :], bank[SLOTS * h + j][:], vec_column(MEAN_ROW + h, j)
            if engine == "vector":
                nc.vector.tensor_scalar(out=out, in0=acc, scalar1=offset, scalar2=None, op0=ALU.add)
            else:
                nc.scalar.activation(out=out, in_=acc, func=ACT.Identity, bias=offset)

        def interleave_stat(stat, h, segs):
            interleave("vector", stat_mixed[stat, h][:, segs, :], stat_rows[stat, h][:, :, segs])

        def quantize_stat(stat, h, segs):
            mixed = stat_mixed[stat, h][:, segs, :].rearrange("p r j -> p (r j)")
            quantize(stat_codes[stat, h][:, segs], stat_plane[stat, h][:, segs], mixed)

        w_hbm = {"dev": w_dev, "mean": w_mean}
        w_tiles = [(stat, h, e) for stat, h in stat_halves for e in range(2)]
        w_raw = {k: tile("w_raw_%s_%d" % k, [P, SLOTS, E], BF16) for k in stat_halves}
        w_mixed = {k: tile("w_mixed_%s_%d_%d" % k, [P, SLOTS, P, SLOTS], BF16) for k in w_tiles}
        w_codes = {k: tile("w_codes_%s_%d_%d" % k, [P, HALF], U32) for k in w_tiles}
        w_plane = {k: tile("w_plane_%s_%d_%d" % k, [P, HALF], U8) for k in w_tiles}

        def load_w(stat, h):
            rows = w_hbm[stat][HALF * h : HALF * (h + 1), :].rearrange("(q j c) e -> c q j e", j=SLOTS, c=4)
            for c in range(4):
                nc.sync.dma_start(out=w_raw[stat, h][c:P:4, :, :], in_=rows[c])

        def interleave_w(engine, stat, h, e, slots):
            src = w_raw[stat, h][:, :, HALF * e : HALF * (e + 1)].rearrange("p j (m a t) -> p m t a j", a=2, t=SLOTS)
            dst = w_mixed[stat, h, e][:].rearrange("p t (m a) j -> p m t a j", a=2)
            copy_on[engine](out=dst[:, :, slots], in_=src[:, :, slots])

        def quantize_w(stat, h, e):
            mixed = w_mixed[stat, h, e][:].rearrange("p t m j -> p (t m j)")
            quantize(w_codes[stat, h, e][:], w_plane[stat, h, e][:], mixed)

        def embed_pass(e, segs, t, i):
            stat, h = stat_halves[i]
            cols = slice(P * t, P * (t + 1))
            nc.tensor.matmul_mx(
                out=bank[t][:, segs],
                lhsT=w_codes[stat, h, e][:, cols].bitcast(FP8X4), lhsT_scale=w_plane[stat, h, e][:, cols],
                rhs=stat_codes[stat, h][:, segs].bitcast(FP8X4), rhs_scale=stat_plane[stat, h][:, segs],
                start=(i == 0), stop=(i == len(stat_halves) - 1),
            )

        def embed(e, segs, t):
            for i in range(len(stat_halves)):
                embed_pass(e, segs, t, i)

        y_cols_low = tile("y_cols_low", [P, SLOTS, R], F32)
        y_cols_high = [tile("y_cols_high%d" % u, [P, SLOTS, R // 2], F32) for u in range(2)]
        y_mixed = [tile("y_mixed%d" % e, [P, R, SLOTS], BF16) for e in range(2)]
        y_codes = [tile("y_codes%d" % e, [P, R], U32) for e in range(2)]
        y_plane = tile("y_plane", [P, 2, R], U8)
        y_rows = [tile("y_rows%d" % e, [P, R // P, HALF], F32) for e in range(2)]

        def y_cols(e, segs):
            if e == 0:
                return y_cols_low[:, :, segs]
            first = segs.start % (R // 2)
            return y_cols_high[segs.start // (R // 2)][:, :, first : first + segs.stop - segs.start]

        def squash(e, segs, t):
            nc.scalar.activation(
                out=y_cols(e, segs)[:, t, :], in_=bank[t][:, segs], func=ACT.Tanh, bias=vec_column(BIAS_ROW + e, t)
            )

        def apply_gain(engine, e, segs, t):
            y, factor = y_cols(e, segs)[:, t, :], vec_column(GAIN_ROW + e, t)
            if engine == "vector":
                nc.vector.tensor_scalar(out=y, in0=y, scalar1=factor, scalar2=None, op0=ALU.mult)
            else:
                nc.scalar.activation(out=y, in_=y, func=ACT.Copy, scale=factor)

        def interleave_y(e, segs):
            interleave("vector", y_mixed[e][:, segs, :], y_cols(e, segs))

        def quantize_y(e, segs):
            quantize(y_codes[e][:, segs], y_plane[:, e, segs], y_mixed[e][:, segs, :].rearrange("p r t -> p (r t)"))

        def turn(e, block):
            src = y_cols(e, slice(P * block, P * (block + 1)))
            for t in range(SLOTS):
                nc.tensor.transpose(bank[TURN_BANK + block][:, P * t : P * (t + 1)], src[:, t, :], ident[:])

        def unload(engine, e, block):
            copy_on[engine](
                out=y_rows[e][:, block, :].rearrange("r (p t) -> r p t", t=SLOTS),
                in_=bank[TURN_BANK + block][:].rearrange("r (t p) -> r p t", t=SLOTS),
            )

        def store_rows(e, block):
            dst = out_0[P * block : P * (block + 1), HALF * e : HALF * (e + 1)]
            nc.sync.dma_start(out=dst, in_=y_rows[e][:, block, :])

        def store_codes(queue, e, segs):
            dst = out_1[e].rearrange("p m t -> p (m t)").bitcast(I32)
            queue.dma_start(out=dst[:, segs], in_=y_codes[e][:, segs].bitcast(I32))

        def store_plane():
            rows = out_2.rearrange("g (q r) m -> r q g m", r=4)
            for r in range(4):
                nc.sync.dma_start(out=rows[r].bitcast(I32), in_=y_plane[r:P:32, :, :].bitcast(I32))

        make_identity(nc, ident[:])
        nc.vector.memset(pool_plane_raw["dev"][:].bitcast(I32), 0)
        nc.vector.memset(attn_plane[:].bitcast(I32), 0)
        nc.vector.memset(table_warmup[:, 0:1], 1.0)
        nc.vector.memset(vec_ordered[:], 0.0)
        nc.vector.memset(pool_plane_raw["mean"][:].bitcast(I32), 0)
        nc.scalar.activation(out=table_warmup[:, 1:2], in_=table_warmup[:, 0:1], func=ACT.Sqrt)

        load_attn(0, 1)
        load_words("dev", 0, 1)
        load_vectors()
        load_words("dev", 2, 4)
        load_plane(pool_plane_raw["dev"], square_scales)
        load_plane(attn_plane, attn_scales)
        load_w("dev", 0)
        load_words("dev", 1, 2)
        load_attn(1, 2)
        load_w("dev", 1)
        load_attn(2, 4)
        load_words("mean", 0, 2)
        load_plane(pool_plane_raw["mean"], frame_scales)
        load_w("mean", 0)
        load_words("mean", 2, 4)
        load_w("mean", 1)

        spread_vectors()
        order_words("dev", 0, 1)
        unload_vectors()
        order_plane("dev", 0, 1)
        for h, j in feature_groups:
            pool_passes("dev", h, j, 0, 1)
        order_words("dev", 2, 4)
        order_plane("dev", 1, 4)
        interleave_w("vector", "dev", 0, 0, LOW)
        interleave_w("scalar", "dev", 0, 1, LOW)
        order_words("dev", 1, 2)
        for h, j in feature_groups:
            pool_passes("dev", h, j, 1, 2)
        interleave_w("scalar", "dev", 0, 0, HIGH)
        interleave_w("vector", "dev", 0, 1, HIGH)
        quantize_w("dev", 0, 1)
        interleave_w("scalar", "dev", 1, 0, LOW)

        for h, j in feature_groups:
            pool_passes("dev", h, j, 2, 4)
            finish_dev(h, j)
        quantize_w("dev", 0, 0)
        interleave_w("vector", "dev", 1, 1, BOTH)
        interleave_w("vector", "dev", 1, 0, HIGH)
        quantize_w("dev", 1, 1)
        order_words("mean", 0, 2)
        order_plane("mean", 0, 4)
        quantize_w("dev", 1, 0)

        for g in range(2):
            for h, j in feature_groups:
                pool_passes("mean", h, j, g, g + 1)
        interleave_stat("dev", 0, ALL)
        interleave_w("scalar", "mean", 0, 0, LOW)
        interleave_w("vector", "mean", 0, 0, HIGH)
        order_words("mean", 2, 4)
        interleave_w("scalar", "mean", 0, 1, LOW)
        quantize_stat("dev", 0, ALL)
        interleave_stat("dev", 1, FIRST)
        quantize_w("mean", 0, 0)
        interleave_w("scalar", "mean", 1, 0, LOW)
        interleave_w("vector", "mean", 1, 0, HIGH)
        interleave_stat("dev", 1, SECOND)
        interleave_w("vector", "mean", 1, 1, LOW)
        quantize_w("mean", 1, 0)
        quantize_stat("dev", 1, ALL)

        for h, j in feature_groups:
            pool_passes("mean", h, j, 2, 4)
            finish_mean("vector" if (h, j) == (1, 0) else "scalar", h, j)
        for h in range(2):
            for segs in (FIRST, SECOND):
                interleave_stat("mean", h, segs)
            for segs in (FIRST, SECOND):
                quantize_stat("mean", h, segs)
        interleave_w("scalar", "mean", 0, 1, HIGH)
        interleave_w("vector", "mean", 1, 1, HIGH)
        quantize_w("mean", 0, 1)
        quantize_w("mean", 1, 1)

        for i in range(len(stat_halves)):
            for t in range(SLOTS):
                embed_pass(0, ALL, t, i)
        for t in range(SLOTS):
            squash(0, ALL, t)
            apply_gain("vector", 0, ALL, t)

        for t in range(SLOTS):
            embed(1, FIRST, t)
            squash(1, FIRST, t)
        for block in range(R // P):
            turn(0, block)
        apply_gain("vector", 1, FIRST, 0)
        interleave_y(0, FIRST)
        apply_gain("vector", 1, FIRST, 1)
        quantize_y(0, FIRST)
        store_codes(nc.sync, 0, FIRST)
        interleave_y(0, SECOND)
        apply_gain("vector", 1, FIRST, 2)
        quantize_y(0, SECOND)
        for block in range(2):
            unload("scalar", 0, block)
            store_rows(0, block)
        store_codes(nc.sync, 0, SECOND)
        apply_gain("scalar", 1, FIRST, 3)
        unload("vector", 0, 2)
        store_rows(0, 2)

        for t in range(SLOTS):
            embed(1, SECOND, t)
        interleave_y(1, FIRST)
        squash(1, SECOND, 0)
        unload("scalar", 0, 3)
        store_rows(0, 3)
        apply_gain("vector", 1, SECOND, 0)
        quantize_y(1, FIRST)
        for t in range(1, SLOTS):
            squash(1, SECOND, t)
        for t in range(1, SLOTS - 1):
            apply_gain("vector", 1, SECOND, t)
        store_codes(nc.scalar, 1, FIRST)
        apply_gain("scalar", 1, SECOND, SLOTS - 1)
        for block in range(R // P):
            turn(1, block)
        unload("vector", 1, 0)
        store_rows(1, 0)
        interleave_y(1, SECOND)
        quantize_y(1, SECOND)
        for block in range(1, R // P - 1):
            unload("scalar", 1, block)
            store_rows(1, block)
        store_codes(nc.sync, 1, SECOND)
        unload("scalar", 1, R // P - 1)
        store_rows(1, R // P - 1)
        store_plane()
